import numpy as np
import ml_dtypes


def mxq(x, axis, fmt="e4m3"):
    dtype, down = {"e4m3": (ml_dtypes.float8_e4m3fn, 7), "e5m2": (ml_dtypes.float8_e5m2, 14)}[fmt]
    v = np.moveaxis(np.asarray(x, np.float32).astype(ml_dtypes.bfloat16).astype(np.float64), axis, -1)
    blocks = v.reshape(v.shape[:-1] + (-1, 32))
    amax = np.abs(blocks).max(-1, keepdims=True)
    byte = np.maximum(np.where(amax > 0, np.frexp(amax)[1] - 1 + 127, 0) - down, 1)
    scale = np.exp2(byte - 127.0)
    codes = (blocks / scale).astype(np.float32).astype(dtype).astype(np.float64)
    return np.moveaxis((codes * scale).reshape(v.shape), -1, axis)


WIDE = False


def mx_kscale(k):
    if not WIDE:
        return np.ones(k)
    levels = np.array([10, -10, 5, -5, 0])
    if k % 512:
        return np.exp2(np.random.permutation(np.resize(levels, k // 32))).repeat(32)
    a = np.empty((k // 512, 16))
    for p in range(k // 512):
        a[p, :8] = np.random.permutation(np.resize(levels, 8))
        for g in range(8):
            far = levels[np.abs(levels - a[p, g]) >= 10]
            a[p, g + 8] = far[np.random.randint(len(far))]
    return np.exp2(a.ravel()).repeat(32)


def f64(x):
    return np.asarray(x).astype(np.float64)


def striped(idx):
    return np.tile(np.asarray(idx).reshape(-1, 16).T, (8, 1)).astype(np.uint16)


def unstriped(offs):
    return offs[:16].T.reshape(-1).astype(np.int64)


E2M1 = np.array([0.0, 0.5, 1.0, 1.5, 2.0, 3.0, 4.0, 6.0, -0.0, -0.5, -1.0, -1.5, -2.0, -3.0, -4.0, -6.0])


def pack_weight(w, fmt):
    k, n = w.shape
    w = f64(np.asarray(w, np.float32).astype(ml_dtypes.bfloat16)).reshape(k // 32, 32, n)
    amax = np.abs(w).max(1)
    if fmt == "e4m3":
        byte = np.frexp(amax)[1] - 1 + 127 - 7
    else:
        mant, ex = np.frexp(amax / 6.0)
        byte = np.where(mant > 0.5, ex, ex - 1) + 127
    byte = np.clip(np.where(amax > 0, byte, 1), 1, 254)
    scaled = (w * np.exp2(127.0 - byte)[:, None, :]).reshape(k, n).astype(np.float32)
    by_word = np.ascontiguousarray(scaled.reshape(k // 512, 128, 4, n).transpose(0, 1, 3, 2))
    if fmt == "e4m3":
        words = by_word.astype(ml_dtypes.float8_e4m3fn).view(np.uint8)
    else:
        c = by_word.astype(ml_dtypes.float4_e2m1fn).view(np.uint8) & 0xF
        words = (c[..., 0::2] | (c[..., 1::2] << 4)).reshape(k // 512, 128, 2 * n)
    return np.ascontiguousarray(words), np.ascontiguousarray(byte.astype(np.uint8).reshape(k // 512, 16, n))


def unpack_weight(words, scales, fmt):
    g, _, n = scales.shape
    words = np.ascontiguousarray(words).reshape(g, 128, n, -1)
    if fmt == "e4m3":
        vals = words.view(ml_dtypes.float8_e4m3fn).astype(np.float64)
    else:
        nib = np.empty((g, 128, n, 4), np.uint8)
        nib[..., 0::2] = words & 0xF
        nib[..., 1::2] = words >> 4
        vals = E2M1[nib]
    vals = vals * np.repeat(np.exp2(scales.astype(np.float64) - 127.0), 8, axis=1)[..., None]
    return vals.transpose(0, 1, 3, 2).reshape(g * 512, n)


def bf(x):
    return np.asarray(x, np.float32).astype(ml_dtypes.bfloat16)


def planes(Y):
    r, m = Y.shape
    b = f64(bf(Y)).reshape(r // 32, 32, m)
    amax = np.abs(b).max(1)
    byte = np.clip(np.where(amax > 0, np.frexp(amax)[1] - 1 + 127 - 7, 1), 1, 254)
    codes = (b * np.exp2(127.0 - byte)[:, None, :]).reshape(r, m).astype(np.float32).astype(ml_dtypes.float8_e4m3fn).view(np.uint8)
    words = codes.reshape(r // 512, 128, 4, m).transpose(0, 1, 3, 2)
    return np.ascontiguousarray(words), np.ascontiguousarray(byte.astype(np.uint8).reshape(r // 512, 16, m))


B, N, T, D, NQ = 1, 512, 2048, 512, 512


def setup_inputs():
    n = np.random.standard_normal
    idx = np.random.permutation(T)[:B * N]
    s = mx_kscale(D)[:, None]
    kp = pack_weight(n((D, T)) / s, "e4m3")
    return {
        "qT": (n((B, D, NQ)) * s * (1.00 / np.sqrt(D))).astype(np.float32),
        "k_words": kp[0],
        "k_scales": kp[1],
        "kb": np.tile(n(2048), (128, 1)).astype(np.float32),
        "ls": (np.random.uniform(7.8, 8.4, (B, 1, NQ))).astype(np.float32),
        "offs": striped(idx),
    }


def reference(qT, k_words, k_scales, kb, ls, offs):
    idx = unstriped(offs)
    pick = lambda x, which: x[:, which].reshape(x.shape[0], B, -1).transpose(1, 0, 2)
    k = unpack_weight(k_words, k_scales, "e4m3")
    kg = pick(k, idx)
    qq = mxq(f64(qT), 1, "e4m3")
    a = kg.transpose(0, 2, 1) @ qq
    y = np.exp(a + pick(f64(kb), idx)[:, :1, :].transpose(0, 2, 1) - f64(ls))
    Y = y[0]
    words, scales = planes(Y)
    return Y, words, scales

@@ -1,0 +1,174 @@
+from contextlib import ExitStack
+
+import concourse.mybir as mybir
+from concourse.masks import make_identity
+
+N, T, D, NQ = 512, 2048, 512, 512
+FLOPS = 2 * N * D * NQ
+BYTES = 4 * D * NQ + D * T + 16 * T + 4 * T + 4 * NQ + 2 * 128 * (N // 16) + 4 * N * NQ + N * NQ + 16 * NQ
+
+F32 = mybir.dt.float32
+BF16 = mybir.dt.bfloat16
+I32 = mybir.dt.int32
+U32 = mybir.dt.uint32
+U16 = mybir.dt.uint16
+U8 = mybir.dt.uint8
+FP8X4 = mybir.dt.float8_e4m3fn_x4
+ACT = mybir.ActivationFunctionType
+ALU = mybir.AluOpType
+
+P = 128
+PACK = 4
+CHUNK = 128
+AT_SCALES, AT_WORDS, AT_LS, AT_X0 = 0, 2048, 10240, 16384
+
+
+def tile_attend_plw_kb_topk_kernel(tc, qT, k_words, k_scales, kb, ls, offs, out_0, out_1, out_2):
+    nc = tc.nc
+    chunks = NQ // CHUNK
+    with ExitStack() as ctx:
+        sb = ctx.enter_context(tc.tile_pool(name="sb", bufs=1))
+        shared = ctx.enter_context(tc.tile_pool(name="shared", bufs=1))
+        ps = ctx.enter_context(tc.psum_pool(name="ps", bufs=1))
+
+        def placed(shape, dtype, name, at):
+            if at is None:
+                return sb.tile(shape, dtype, name=name, align_bytes=64)
+            return shared.tile(shape, dtype, name=name, align_bytes=64, offset=at)
+
+        offsets = sb.tile([P, N // 16], U16, name="offsets")
+        nc.sync.dma_start(offsets[:], offs)
+        ls_rows = placed([P, PACK], F32, "ls_rows", AT_LS)
+        nc.sync.dma_start(ls_rows[:], ls[0, 0].rearrange("(p j) -> p j", j=PACK))
+        q_rows = qT[0].rearrange("(p t) q -> p t q", t=PACK)
+        q_first = sb.tile([P, PACK, CHUNK], F32, name="q_first")
+        nc.sync.dma_start(q_first[:], q_rows[:, :, 0:CHUNK])
+
+        scale_pool = placed([P, T], U8, "scale_pool", AT_SCALES)
+        nc.vector.memset(scale_pool[:].bitcast(I32), 0)
+        for quad in range(4):
+            nc.scalar.dma_start(
+                scale_pool[32 * quad : 32 * quad + 4, :].bitcast(I32),
+                k_scales[0, 4 * quad : 4 * quad + 4, :].bitcast(I32),
+            )
+
+        kb_pool = sb.tile([P, T], F32, name="kb_pool")
+        nc.vector.memset(kb_pool[:].bitcast(I32), 0)
+        nc.sync.dma_start(kb_pool[0:1, :], kb[0:1, :])
+
+        zeros = placed([P, P], F32, "zeros", AT_WORDS)
+        nc.vector.memset(zeros[:], 0.0)
+        ident = sb.tile([P, P], F32, name="ident")
+        nc.gpsimd.affine_select(
+            out=ident[:],
+            in_=zeros[:],
+            compare_op=ALU.not_equal,
+            fill=1.0,
+            base=0,
+            pattern=[[-1, P]],
+            channel_multiplier=1,
+        )
+        word_pool = placed([P, T], I32, "word_pool", AT_WORDS)
+        nc.sync.dma_start(word_pool[:], k_words[0].rearrange("p t r -> p (t r)").bitcast(I32))
+
+        ls_ps = ps.tile([P, PACK, P], F32, name="ls_ps")
+        for j in range(PACK):
+            nc.tensor.transpose(ls_ps[:, j, :], ls_rows[:, j : j + 1].to_broadcast([P, P]), ident[:])
+        q_rest = placed([P, chunks - 1, PACK, CHUNK], F32, "q_rest", AT_LS)
+        for c in range(1, chunks):
+            nc.sync.dma_start(q_rest[:, c - 1], q_rows[:, :, c * CHUNK : (c + 1) * CHUNK])
+        q_raw = [q_first[:]] + [q_rest[:, c] for c in range(chunks - 1)]
+        ls_all = sb.tile([P, NQ], F32, name="ls_all")
+        nc.scalar.activation(
+            ls_all[:].rearrange("p (c j) -> p c j", j=PACK), ls_ps[:].rearrange("p j c -> p c j"), ACT.Copy
+        )
+
+        scale_got = placed([P, N], U8, "scale_got", None)
+        nc.vector.tensor_copy(scale_got[:], scale_pool[:].indirect(offsets[:]))
+        k_sc = placed([P, N], U8, "k_sc", None)
+        nc.vector.tensor_copy(
+            k_sc[:].rearrange("p (r s) -> p r s", r=PACK), scale_got[:].rearrange("p (s r) -> p r s", r=PACK)
+        )
+
+        kb_got = sb.tile([P, N], F32, name="kb_got")
+        nc.vector.tensor_copy(kb_got[:], kb_pool[:].indirect(offsets[:]))
+        kb_ps = ps.tile([P, PACK, P], F32, name="kb_ps")
+        for r in range(PACK):
+            nc.tensor.transpose(kb_ps[:, r, :], kb_got[:, r::PACK], ident[:])
+        kb_col = sb.tile([P, PACK], F32, name="kb_col")
+        nc.scalar.copy(kb_col[:], kb_ps[:, :, 0])
+
+        y_rows = out_0.rearrange("(p r) q -> p r q", r=PACK)
+        y_words = out_1[0].rearrange("p q u -> p (q u)").bitcast(I32)
+        y_sc = placed([P, NQ], U8, "y_sc", None)
+        k_codes = placed([P, N], U32, "k_codes", None)
+        q_mx = {}
+        y_f32 = {}
+
+        def quantise_queries(c):
+            q_bf = placed([P, CHUNK, PACK], BF16, "q_bf%d" % c, AT_X0 if c == 1 else None)
+            nc.scalar.activation(
+                q_bf[:].rearrange("p (c i) t -> p c t i", i=4),
+                q_raw[c].rearrange("p t (c i) -> p c t i", i=4),
+                ACT.Copy,
+            )
+            q_codes = placed([P, CHUNK], U32, "q_codes%d" % c, AT_SCALES if c == 0 else None)
+            q_sc = placed([P, CHUNK], U8, "q_sc%d" % c, None)
+            nc.vector.quantize_mx(
+                out=q_codes[:].bitcast(FP8X4), scales=q_sc[:], in_=q_bf[:].rearrange("p q t -> p (q t)")
+            )
+            q_mx[c] = (q_codes, q_sc)
+
+        def weigh(c):
+            cols = slice(c * CHUNK, (c + 1) * CHUNK)
+            q_codes, q_sc = q_mx[c]
+            score = ps.tile([P, PACK, CHUNK], F32, name="score%d" % c)
+            for r in range(PACK):
+                slots = slice(r * P, (r + 1) * P)
+                nc.tensor.matmul_mx(
+                    out=score[:, r, :],
+                    lhsT=k_codes[:, slots].bitcast(FP8X4),
+                    lhsT_scale=k_sc[:, slots],
+                    rhs=q_codes[:].bitcast(FP8X4),
+                    rhs_scale=q_sc[:],
+                    start=True,
+                    stop=True,
+                )
+            x = placed([P, PACK, CHUNK], F32, "x%d" % c, AT_X0 if c == 0 else None)
+            nc.vector.tensor_tensor(
+                x[:], score[:], ls_all[:, cols].unsqueeze(1).to_broadcast([P, PACK, CHUNK]), ALU.subtract
+            )
+            y = sb.tile([P, PACK, CHUNK], F32, name="y%d" % c)
+            for r in range(PACK):
+                nc.scalar.activation(y[:, r, :], x[:, r, :], ACT.Exp, bias=kb_col[:, r : r + 1])
+            nc.sync.dma_start(y_rows[:, :, cols], y[:])
+            y_f32[c] = y
+
+        def hand_on(c):
+            cols = slice(c * CHUNK, (c + 1) * CHUNK)
+            y_bf = placed([P, CHUNK, PACK], BF16, "y_bf%d" % c, None)
+            nc.vector.tensor_copy(
+                y_bf[:].rearrange("p (c i) r -> p c r i", i=4), y_f32[c][:].rearrange("p r (c i) -> p c r i", i=4)
+            )
+            y_codes = placed([P, CHUNK], U32, "y_codes%d" % c, None)
+            nc.vector.quantize_mx(
+                out=y_codes[:].bitcast(FP8X4), scales=y_sc[:, cols], in_=y_bf[:].rearrange("p q r -> p (q r)")
+            )
+            nc.sync.dma_start(y_words[:, cols], y_codes[:].bitcast(I32))
+
+        quantise_queries(0)
+        nc.vector.tensor_copy(
+            k_codes[:].rearrange("p (r s) -> p s r", r=PACK), word_pool[:].bitcast(U32).indirect(offsets[:])
+        )
+        for c in range(chunks):
+            if c + 1 < chunks:
+                quantise_queries(c + 1)
+            weigh(c)
+        for c in range(chunks):
+            hand_on(c)
+        for quad in range(4):
+            queue = nc.sync if quad % 2 else nc.scalar
+            queue.dma_start(
+                out_2[0, 4 * quad : 4 * quad + 4, :].bitcast(I32),
+                y_sc[32 * quad : 32 * quad + 4, :].bitcast(I32),
+            )

@@ -19,30 +19,36 @@ ALU = mybir.AluOpType
 
 P = 128
 PACK = 4
+HALF = 256
 CHUNK = 128
-AT_SCALES, AT_WORDS, AT_LS, AT_X0 = 0, 2048, 10240, 16384
+AT_SCALES, AT_WORDS, AT_LS, AT_LATE_BF = 0, 2048, 10240, 14336
 
 
 def tile_attend_plw_kb_topk_kernel(tc, qT, k_words, k_scales, kb, ls, offs, out_0, out_1, out_2):
     nc = tc.nc
-    chunks = NQ // CHUNK
     with ExitStack() as ctx:
         sb = ctx.enter_context(tc.tile_pool(name="sb", bufs=1))
         shared = ctx.enter_context(tc.tile_pool(name="shared", bufs=1))
         ps = ctx.enter_context(tc.psum_pool(name="ps", bufs=1))
 
-        def placed(shape, dtype, name, at):
+        def placed(shape, dtype, name, at=None):
             if at is None:
                 return sb.tile(shape, dtype, name=name, align_bytes=64)
             return shared.tile(shape, dtype, name=name, align_bytes=64, offset=at)
+
+        def woven(words):
+            return words.rearrange("p (c i) t -> p c t i", i=4)
+
+        def by_rows(rows):
+            return rows.rearrange("p t (c i) -> p c t i", i=4)
 
         offsets = sb.tile([P, N // 16], U16, name="offsets")
         nc.sync.dma_start(offsets[:], offs)
         ls_rows = placed([P, PACK], F32, "ls_rows", AT_LS)
         nc.sync.dma_start(ls_rows[:], ls[0, 0].rearrange("(p j) -> p j", j=PACK))
         q_rows = qT[0].rearrange("(p t) q -> p t q", t=PACK)
-        q_first = sb.tile([P, PACK, CHUNK], F32, name="q_first")
-        nc.sync.dma_start(q_first[:], q_rows[:, :, 0:CHUNK])
+        q_first = placed([P, PACK, HALF], F32, "q_first")
+        nc.sync.dma_start(q_first[:], q_rows[:, :, 0:HALF])
 
         scale_pool = placed([P, T], U8, "scale_pool", AT_SCALES)
         nc.vector.memset(scale_pool[:].bitcast(I32), 0)
@@ -52,13 +58,13 @@ def tile_attend_plw_kb_topk_kernel(tc, qT, k_words, k_scales, kb, ls, offs, out_
                 k_scales[0, 4 * quad : 4 * quad + 4, :].bitcast(I32),
             )
 
-        kb_pool = sb.tile([P, T], F32, name="kb_pool")
+        kb_pool = placed([P, T], F32, "kb_pool")
         nc.vector.memset(kb_pool[:].bitcast(I32), 0)
         nc.sync.dma_start(kb_pool[0:1, :], kb[0:1, :])
 
         zeros = placed([P, P], F32, "zeros", AT_WORDS)
         nc.vector.memset(zeros[:], 0.0)
-        ident = sb.tile([P, P], F32, name="ident")
+        ident = placed([P, P], F32, "ident")
         nc.gpsimd.affine_select(
             out=ident[:],
             in_=zeros[:],
@@ -74,100 +80,91 @@ def tile_attend_plw_kb_topk_kernel(tc, qT, k_words, k_scales, kb, ls, offs, out_
         ls_ps = ps.tile([P, PACK, P], F32, name="ls_ps")
         for j in range(PACK):
             nc.tensor.transpose(ls_ps[:, j, :], ls_rows[:, j : j + 1].to_broadcast([P, P]), ident[:])
-        q_rest = placed([P, chunks - 1, PACK, CHUNK], F32, "q_rest", AT_LS)
-        for c in range(1, chunks):
-            nc.sync.dma_start(q_rest[:, c - 1], q_rows[:, :, c * CHUNK : (c + 1) * CHUNK])
-        q_raw = [q_first[:]] + [q_rest[:, c] for c in range(chunks - 1)]
-        ls_all = sb.tile([P, NQ], F32, name="ls_all")
+        q_rest = placed([P, 2, PACK, CHUNK], F32, "q_rest", AT_LS)
+        for c in range(2):
+            nc.sync.dma_start(q_rest[:, c], q_rows[:, :, HALF + c * CHUNK : HALF + (c + 1) * CHUNK])
+        ls_all = placed([P, NQ], F32, "ls_all")
         nc.scalar.activation(
             ls_all[:].rearrange("p (c j) -> p c j", j=PACK), ls_ps[:].rearrange("p j c -> p c j"), ACT.Copy
         )
 
-        scale_got = placed([P, N], U8, "scale_got", None)
+        scale_got = placed([P, N], U8, "scale_got")
         nc.vector.tensor_copy(scale_got[:], scale_pool[:].indirect(offsets[:]))
-        k_sc = placed([P, N], U8, "k_sc", None)
+        k_sc = placed([P, N], U8, "k_sc")
         nc.vector.tensor_copy(
             k_sc[:].rearrange("p (r s) -> p r s", r=PACK), scale_got[:].rearrange("p (s r) -> p r s", r=PACK)
         )
 
-        kb_got = sb.tile([P, N], F32, name="kb_got")
+        kb_got = placed([P, N], F32, "kb_got")
         nc.vector.tensor_copy(kb_got[:], kb_pool[:].indirect(offsets[:]))
         kb_ps = ps.tile([P, PACK, P], F32, name="kb_ps")
         for r in range(PACK):
             nc.tensor.transpose(kb_ps[:, r, :], kb_got[:, r::PACK], ident[:])
-        kb_col = sb.tile([P, PACK], F32, name="kb_col")
+        kb_col = placed([P, PACK], F32, "kb_col")
         nc.scalar.copy(kb_col[:], kb_ps[:, :, 0])
 
-        y_rows = out_0.rearrange("(p r) q -> p r q", r=PACK)
-        y_words = out_1[0].rearrange("p q u -> p (q u)").bitcast(I32)
-        y_sc = placed([P, NQ], U8, "y_sc", None)
-        k_codes = placed([P, N], U32, "k_codes", None)
-        q_mx = {}
-        y_f32 = {}
-
-        def quantise_queries(c):
-            q_bf = placed([P, CHUNK, PACK], BF16, "q_bf%d" % c, AT_X0 if c == 1 else None)
-            nc.scalar.activation(
-                q_bf[:].rearrange("p (c i) t -> p c t i", i=4),
-                q_raw[c].rearrange("p t (c i) -> p c t i", i=4),
-                ACT.Copy,
-            )
-            q_codes = placed([P, CHUNK], U32, "q_codes%d" % c, AT_SCALES if c == 0 else None)
-            q_sc = placed([P, CHUNK], U8, "q_sc%d" % c, None)
+        def quantise_queries(pieces, name, at, at_bf=None):
+            q_bf = placed([P, HALF, PACK], BF16, "q_bf" + name, at_bf)
+            width = HALF // len(pieces)
+            for i, raw in enumerate(pieces):
+                nc.scalar.activation(woven(q_bf[:, i * width : (i + 1) * width, :]), by_rows(raw), ACT.Copy)
+            q_codes = placed([P, HALF], U32, "q_codes" + name, at)
+            q_sc = placed([P, HALF], U8, "q_sc" + name)
             nc.vector.quantize_mx(
                 out=q_codes[:].bitcast(FP8X4), scales=q_sc[:], in_=q_bf[:].rearrange("p q t -> p (q t)")
             )
-            q_mx[c] = (q_codes, q_sc)
+            return q_codes, q_sc
 
-        def weigh(c):
-            cols = slice(c * CHUNK, (c + 1) * CHUNK)
-            q_codes, q_sc = q_mx[c]
-            score = ps.tile([P, PACK, CHUNK], F32, name="score%d" % c)
+        y_rows = out_0.rearrange("(p r) q -> p r q", r=PACK)
+        y_words = out_1[0].rearrange("p q u -> p (q u)").bitcast(I32)
+        y_codes = placed([P, NQ], U32, "y_codes")
+        y_sc = placed([P, NQ], U8, "y_sc")
+
+        def weigh(q_mx, cols, name, at_y=None, at_second=None):
+            y = placed([P, PACK, HALF], F32, "y" + name, at_y)
             for r in range(PACK):
                 slots = slice(r * P, (r + 1) * P)
+                score = ps.tile([P, HALF], F32, name="score", bufs=6)
                 nc.tensor.matmul_mx(
-                    out=score[:, r, :],
+                    out=score[:],
                     lhsT=k_codes[:, slots].bitcast(FP8X4),
                     lhsT_scale=k_sc[:, slots],
-                    rhs=q_codes[:].bitcast(FP8X4),
-                    rhs_scale=q_sc[:],
+                    rhs=q_mx[0][:].bitcast(FP8X4),
+                    rhs_scale=q_mx[1][:],
                     start=True,
                     stop=True,
                 )
-            x = placed([P, PACK, CHUNK], F32, "x%d" % c, AT_X0 if c == 0 else None)
-            nc.vector.tensor_tensor(
-                x[:], score[:], ls_all[:, cols].unsqueeze(1).to_broadcast([P, PACK, CHUNK]), ALU.subtract
-            )
-            y = sb.tile([P, PACK, CHUNK], F32, name="y%d" % c)
-            for r in range(PACK):
-                nc.scalar.activation(y[:, r, :], x[:, r, :], ACT.Exp, bias=kb_col[:, r : r + 1])
-            nc.sync.dma_start(y_rows[:, :, cols], y[:])
-            y_f32[c] = y
+                x = placed([P, HALF], F32, "x%s%d" % (name, r), at_second if r == 1 else None)
+                nc.vector.tensor_tensor(x[:], score[:], ls_all[:, cols], ALU.subtract)
+                nc.scalar.activation(y[:, r, :], x[:], ACT.Exp, bias=kb_col[:, r : r + 1])
+                nc.sync.dma_start(y_rows[:, r, cols], y[:, r, :])
+            return y
 
-        def hand_on(c):
-            cols = slice(c * CHUNK, (c + 1) * CHUNK)
-            y_bf = placed([P, CHUNK, PACK], BF16, "y_bf%d" % c, None)
-            nc.vector.tensor_copy(
-                y_bf[:].rearrange("p (c i) r -> p c r i", i=4), y_f32[c][:].rearrange("p r (c i) -> p c r i", i=4)
-            )
-            y_codes = placed([P, CHUNK], U32, "y_codes%d" % c, None)
+        def quantise_weights(y_bf, cols):
             nc.vector.quantize_mx(
-                out=y_codes[:].bitcast(FP8X4), scales=y_sc[:, cols], in_=y_bf[:].rearrange("p q r -> p (q r)")
+                out=y_codes[:, cols].bitcast(FP8X4), scales=y_sc[:, cols], in_=y_bf[:].rearrange("p q r -> p (q r)")
             )
-            nc.sync.dma_start(y_words[:, cols], y_codes[:].bitcast(I32))
+            nc.sync.dma_start(y_words[:, cols], y_codes[:, cols].bitcast(I32))
 
-        quantise_queries(0)
+        early, late = slice(0, HALF), slice(HALF, NQ)
+        q_early = quantise_queries([q_first[:]], "_early", AT_SCALES)
+        k_codes = placed([P, N], U32, "k_codes")
         nc.vector.tensor_copy(
             k_codes[:].rearrange("p (r s) -> p s r", r=PACK), word_pool[:].bitcast(U32).indirect(offsets[:])
         )
-        for c in range(chunks):
-            if c + 1 < chunks:
-                quantise_queries(c + 1)
-            weigh(c)
-        for c in range(chunks):
-            hand_on(c)
+        q_late = quantise_queries([q_rest[:, 0], q_rest[:, 1]], "_late", AT_WORDS, AT_LATE_BF)
+        y_early = weigh(q_early, early, "_early", AT_LS, AT_LATE_BF)
+        y_late = weigh(q_late, late, "_late")
+
+        early_bf = placed([P, HALF, PACK], BF16, "early_bf")
+        late_bf = placed([P, HALF, PACK], BF16, "late_bf")
+        nc.vector.tensor_copy(woven(early_bf[:]), by_rows(y_early[:]))
+        nc.vector.tensor_copy(woven(late_bf[:, 0:CHUNK, :]), by_rows(y_late[:, :, 0:CHUNK]))
+        nc.scalar.activation(woven(late_bf[:, CHUNK:, :]), by_rows(y_late[:, :, CHUNK:]), ACT.Copy)
+        quantise_weights(early_bf, early)
+        quantise_weights(late_bf, late)
         for quad in range(4):
-            queue = nc.sync if quad % 2 else nc.scalar
+            queue = nc.sync if quad == 3 else nc.scalar
             queue.dma_start(
                 out_2[0, 4 * quad : 4 * quad + 4, :].bitcast(I32),
                 y_sc[32 * quad : 32 * quad + 4, :].bitcast(I32),

@@ -21,7 +21,8 @@ P = 128
 PACK = 4
 HALF = 256
 CHUNK = 128
-AT_SCALES, AT_WORDS, AT_LS, AT_LATE_BF = 0, 2048, 10240, 14336
+AT_SCALES, AT_KB, AT_ZEROS, AT_SCALE_GOT, AT_WORDS = 0, 2048, 10112, 10240, 10752
+AT_LS, AT_LATE_BF = 18944, 23104
 
 
 def tile_attend_plw_kb_topk_kernel(tc, qT, k_words, k_scales, kb, ls, offs, out_0, out_1, out_2):
@@ -53,21 +54,17 @@ def tile_attend_plw_kb_topk_kernel(tc, qT, k_words, k_scales, kb, ls, offs, out_
         scale_pool = placed([P, T], U8, "scale_pool", AT_SCALES)
         nc.vector.memset(scale_pool[:].bitcast(I32), 0)
         for quad in range(4):
-            nc.scalar.dma_start(
+            nc.sync.dma_start(
                 scale_pool[32 * quad : 32 * quad + 4, :].bitcast(I32),
                 k_scales[0, 4 * quad : 4 * quad + 4, :].bitcast(I32),
             )
 
-        kb_pool = placed([P, T], F32, "kb_pool")
-        nc.vector.memset(kb_pool[:].bitcast(I32), 0)
-        nc.sync.dma_start(kb_pool[0:1, :], kb[0:1, :])
-
-        zeros = placed([P, P], F32, "zeros", AT_WORDS)
-        nc.vector.memset(zeros[:], 0.0)
+        zeros = placed([P, 192], F32, "zeros", AT_ZEROS)
+        nc.vector.memset(zeros[:, 0:P], 0.0)
         ident = placed([P, P], F32, "ident")
         nc.gpsimd.affine_select(
             out=ident[:],
-            in_=zeros[:],
+            in_=zeros[:, 0:P],
             compare_op=ALU.not_equal,
             fill=1.0,
             base=0,
@@ -76,6 +73,9 @@ def tile_attend_plw_kb_topk_kernel(tc, qT, k_words, k_scales, kb, ls, offs, out_
         )
         word_pool = placed([P, T], I32, "word_pool", AT_WORDS)
         nc.sync.dma_start(word_pool[:], k_words[0].rearrange("p t r -> p (t r)").bitcast(I32))
+        kb_pool = placed([P, T], F32, "kb_pool", AT_KB)
+        nc.vector.memset(kb_pool[:].bitcast(I32), 0)
+        nc.sync.dma_start(kb_pool[0:1, :], kb[0:1, :])
 
         ls_ps = ps.tile([P, PACK, P], F32, name="ls_ps")
         for j in range(PACK):
@@ -88,20 +88,12 @@ def tile_attend_plw_kb_topk_kernel(tc, qT, k_words, k_scales, kb, ls, offs, out_
             ls_all[:].rearrange("p (c j) -> p c j", j=PACK), ls_ps[:].rearrange("p j c -> p c j"), ACT.Copy
         )
 
-        scale_got = placed([P, N], U8, "scale_got")
+        scale_got = placed([P, N], U8, "scale_got", AT_SCALE_GOT)
         nc.vector.tensor_copy(scale_got[:], scale_pool[:].indirect(offsets[:]))
         k_sc = placed([P, N], U8, "k_sc")
         nc.vector.tensor_copy(
             k_sc[:].rearrange("p (r s) -> p r s", r=PACK), scale_got[:].rearrange("p (s r) -> p r s", r=PACK)
         )
-
-        kb_got = placed([P, N], F32, "kb_got")
-        nc.vector.tensor_copy(kb_got[:], kb_pool[:].indirect(offsets[:]))
-        kb_ps = ps.tile([P, PACK, P], F32, name="kb_ps")
-        for r in range(PACK):
-            nc.tensor.transpose(kb_ps[:, r, :], kb_got[:, r::PACK], ident[:])
-        kb_col = placed([P, PACK], F32, "kb_col")
-        nc.scalar.copy(kb_col[:], kb_ps[:, :, 0])
 
         def quantise_queries(pieces, name, at, at_bf=None):
             q_bf = placed([P, HALF, PACK], BF16, "q_bf" + name, at_bf)
@@ -120,8 +112,9 @@ def tile_attend_plw_kb_topk_kernel(tc, qT, k_words, k_scales, kb, ls, offs, out_
         y_codes = placed([P, NQ], U32, "y_codes")
         y_sc = placed([P, NQ], U8, "y_sc")
 
-        def weigh(q_mx, cols, name, at_y=None, at_second=None):
-            y = placed([P, PACK, HALF], F32, "y" + name, at_y)
+        def weigh(q_mx, cols, name, at_x=None):
+            x = placed([P, PACK, HALF], F32, "x" + name, at_x)
+            y = placed([P, PACK, HALF], F32, "y" + name)
             for r in range(PACK):
                 slots = slice(r * P, (r + 1) * P)
                 score = ps.tile([P, HALF], F32, name="score", bufs=6)
@@ -134,10 +127,10 @@ def tile_attend_plw_kb_topk_kernel(tc, qT, k_words, k_scales, kb, ls, offs, out_
                     start=True,
                     stop=True,
                 )
-                x = placed([P, HALF], F32, "x%s%d" % (name, r), at_second if r == 1 else None)
-                nc.vector.tensor_tensor(x[:], score[:], ls_all[:, cols], ALU.subtract)
-                nc.scalar.activation(y[:, r, :], x[:], ACT.Exp, bias=kb_col[:, r : r + 1])
-                nc.sync.dma_start(y_rows[:, r, cols], y[:, r, :])
+                nc.vector.tensor_tensor(x[:, r, :], score[:], ls_all[:, cols], ALU.subtract)
+                nc.scalar.activation(y[:, r, :], x[:, r, :], ACT.Exp, bias=kb_col[:, r : r + 1])
+                if r % 2:
+                    nc.sync.dma_start(y_rows[:, r - 1 : r + 1, cols], y[:, r - 1 : r + 1, :])
             return y
 
         def quantise_weights(y_bf, cols):
@@ -152,8 +145,15 @@ def tile_attend_plw_kb_topk_kernel(tc, qT, k_words, k_scales, kb, ls, offs, out_
         nc.vector.tensor_copy(
             k_codes[:].rearrange("p (r s) -> p s r", r=PACK), word_pool[:].bitcast(U32).indirect(offsets[:])
         )
-        q_late = quantise_queries([q_rest[:, 0], q_rest[:, 1]], "_late", AT_WORDS, AT_LATE_BF)
-        y_early = weigh(q_early, early, "_early", AT_LS, AT_LATE_BF)
+        kb_got = placed([P, N], F32, "kb_got", AT_WORDS)
+        nc.vector.tensor_copy(kb_got[:], kb_pool[:].indirect(offsets[:]))
+        kb_ps = ps.tile([P, PACK, P], F32, name="kb_ps")
+        for r in range(PACK):
+            nc.tensor.transpose(kb_ps[:, r, :], kb_got[:, r::PACK], ident[:])
+        kb_col = placed([P, PACK], F32, "kb_col", AT_LS)
+        nc.scalar.copy(kb_col[:], kb_ps[:, :, 0])
+        q_late = quantise_queries([q_rest[:, 0], q_rest[:, 1]], "_late", AT_KB, AT_LATE_BF)
+        y_early = weigh(q_early, early, "_early", AT_LATE_BF)
         y_late = weigh(q_late, late, "_late")
 
         early_bf = placed([P, HALF, PACK], BF16, "early_bf")

@@ -19,10 +19,10 @@ ALU = mybir.AluOpType
 
 P = 128
 PACK = 4
-HALF = 256
 CHUNK = 128
-AT_SCALES, AT_KB, AT_ZEROS, AT_SCALE_GOT, AT_WORDS = 0, 2048, 10112, 10240, 10752
-AT_LS, AT_LATE_BF = 18944, 23104
+CHUNKS = NQ // CHUNK
+KB_ROW = P - 1
+AT_KB_GOT, AT_LS_ROWS = 0, 2048
 
 
 def tile_attend_plw_kb_topk_kernel(tc, qT, k_words, k_scales, kb, ls, offs, out_0, out_1, out_2):
@@ -43,129 +43,117 @@ def tile_attend_plw_kb_topk_kernel(tc, qT, k_words, k_scales, kb, ls, offs, out_
         def by_rows(rows):
             return rows.rearrange("p t (c i) -> p c t i", i=4)
 
+        def columns(c):
+            return slice(c * CHUNK, (c + 1) * CHUNK)
+
+        scale_pool = placed([P, T], U8, "scale_pool")
+        nc.vector.memset(scale_pool[:].bitcast(I32), 0)
+        ident = placed([P, P], F32, "ident")
+        nc.vector.memset(ident[:], 0.0)
+        make_identity(nc, ident[:], nomemset=True)
+        kb_pool = placed([P, T], F32, "kb_pool")
+        nc.vector.memset(kb_pool[0:KB_ROW, :], 0.0)
+
         offsets = sb.tile([P, N // 16], U16, name="offsets")
         nc.sync.dma_start(offsets[:], offs)
-        ls_rows = placed([P, PACK], F32, "ls_rows", AT_LS)
-        nc.sync.dma_start(ls_rows[:], ls[0, 0].rearrange("(p j) -> p j", j=PACK))
+        nc.scalar.dma_start(kb_pool[KB_ROW:P, :], kb[0:1, :])
         q_rows = qT[0].rearrange("(p t) q -> p t q", t=PACK)
-        q_first = placed([P, PACK, HALF], F32, "q_first")
-        nc.sync.dma_start(q_first[:], q_rows[:, :, 0:HALF])
-
-        scale_pool = placed([P, T], U8, "scale_pool", AT_SCALES)
-        nc.vector.memset(scale_pool[:].bitcast(I32), 0)
-        for quad in range(4):
-            nc.sync.dma_start(
-                scale_pool[32 * quad : 32 * quad + 4, :].bitcast(I32),
-                k_scales[0, 4 * quad : 4 * quad + 4, :].bitcast(I32),
-            )
-
-        zeros = placed([P, 192], F32, "zeros", AT_ZEROS)
-        nc.vector.memset(zeros[:, 0:P], 0.0)
-        ident = placed([P, P], F32, "ident")
-        nc.gpsimd.affine_select(
-            out=ident[:],
-            in_=zeros[:, 0:P],
-            compare_op=ALU.not_equal,
-            fill=1.0,
-            base=0,
-            pattern=[[-1, P]],
-            channel_multiplier=1,
-        )
-        word_pool = placed([P, T], I32, "word_pool", AT_WORDS)
+        q_raw = [placed([P, PACK, CHUNK], F32, "q_raw%d" % c) for c in range(CHUNKS)]
+        ls_rows = placed([P, PACK], F32, "ls_rows", AT_LS_ROWS)
+        nc.sync.dma_start(ls_rows[:], ls[0, 0].rearrange("(p j) -> p j", j=PACK))
+        for r in range(4):
+            queue = nc.scalar if r % 2 else nc.sync
+            queue.dma_start(scale_pool[r:P:32, :].bitcast(I32), k_scales[0, r:16:4, :].bitcast(I32))
+        word_pool = placed([P, T], I32, "word_pool")
         nc.sync.dma_start(word_pool[:], k_words[0].rearrange("p t r -> p (t r)").bitcast(I32))
-        kb_pool = placed([P, T], F32, "kb_pool", AT_KB)
-        nc.vector.memset(kb_pool[:].bitcast(I32), 0)
-        nc.sync.dma_start(kb_pool[0:1, :], kb[0:1, :])
+        for c in range(CHUNKS):
+            nc.sync.dma_start(q_raw[c][:], q_rows[:, :, columns(c)])
 
-        ls_ps = ps.tile([P, PACK, P], F32, name="ls_ps")
-        for j in range(PACK):
-            nc.tensor.transpose(ls_ps[:, j, :], ls_rows[:, j : j + 1].to_broadcast([P, P]), ident[:])
-        q_rest = placed([P, 2, PACK, CHUNK], F32, "q_rest", AT_LS)
-        for c in range(2):
-            nc.sync.dma_start(q_rest[:, c], q_rows[:, :, HALF + c * CHUNK : HALF + (c + 1) * CHUNK])
-        ls_all = placed([P, NQ], F32, "ls_all")
-        nc.scalar.activation(
-            ls_all[:].rearrange("p (c j) -> p c j", j=PACK), ls_ps[:].rearrange("p j c -> p c j"), ACT.Copy
-        )
-
-        scale_got = placed([P, N], U8, "scale_got", AT_SCALE_GOT)
+        kb_got = placed([P, N], F32, "kb_got", AT_KB_GOT)
+        nc.vector.tensor_copy(kb_got[:], kb_pool[:].indirect(offsets[:]))
+        scale_got = placed([P, N], U8, "scale_got")
         nc.vector.tensor_copy(scale_got[:], scale_pool[:].indirect(offsets[:]))
         k_sc = placed([P, N], U8, "k_sc")
         nc.vector.tensor_copy(
             k_sc[:].rearrange("p (r s) -> p r s", r=PACK), scale_got[:].rearrange("p (s r) -> p r s", r=PACK)
         )
 
-        def quantise_queries(pieces, name, at, at_bf=None):
-            q_bf = placed([P, HALF, PACK], BF16, "q_bf" + name, at_bf)
-            width = HALF // len(pieces)
-            for i, raw in enumerate(pieces):
-                nc.scalar.activation(woven(q_bf[:, i * width : (i + 1) * width, :]), by_rows(raw), ACT.Copy)
-            q_codes = placed([P, HALF], U32, "q_codes" + name, at)
-            q_sc = placed([P, HALF], U8, "q_sc" + name)
+        ls_ps = ps.tile([P, PACK, P], F32, name="ls_ps")
+        for j in range(PACK):
+            nc.tensor.transpose(ls_ps[:, j, :], ls_rows[:, j : j + 1].to_broadcast([P, P]), ident[:])
+        ls_all = placed([P, NQ], F32, "ls_all")
+        nc.scalar.activation(
+            ls_all[:].rearrange("p (c j) -> p c j", j=PACK), ls_ps[:].rearrange("p j c -> p c j"), ACT.Copy
+        )
+        kb_ps = ps.tile([P, PACK, P], F32, name="kb_ps")
+        for r in range(PACK):
+            nc.tensor.transpose(kb_ps[:, r, :], kb_got[:, r::PACK], ident[:])
+        kb_col = placed([P, PACK], F32, "kb_col")
+        nc.scalar.copy(kb_col[:], kb_ps[:, :, KB_ROW])
+
+        k_codes = placed([P, N], U32, "k_codes")
+        nc.vector.tensor_copy(
+            k_codes[:].rearrange("p (r s) -> p s r", r=PACK), word_pool[:].bitcast(U32).indirect(offsets[:])
+        )
+
+        q_bf = placed([P, NQ, PACK], BF16, "q_bf", AT_KB_GOT)
+        q_codes = placed([P, NQ], U32, "q_codes")
+        q_sc = placed([P, NQ], U8, "q_sc")
+        for c in range(CHUNKS):
+            nc.scalar.activation(woven(q_bf[:, columns(c), :]), by_rows(q_raw[c][:]), ACT.Copy)
             nc.vector.quantize_mx(
-                out=q_codes[:].bitcast(FP8X4), scales=q_sc[:], in_=q_bf[:].rearrange("p q t -> p (q t)")
+                out=q_codes[:, columns(c)].bitcast(FP8X4),
+                scales=q_sc[:, columns(c)],
+                in_=q_bf[:, columns(c), :].rearrange("p q t -> p (q t)"),
             )
-            return q_codes, q_sc
 
         y_rows = out_0.rearrange("(p r) q -> p r q", r=PACK)
         y_words = out_1[0].rearrange("p q u -> p (q u)").bitcast(I32)
         y_codes = placed([P, NQ], U32, "y_codes")
         y_sc = placed([P, NQ], U8, "y_sc")
 
-        def weigh(q_mx, cols, name, at_x=None):
-            x = placed([P, PACK, HALF], F32, "x" + name, at_x)
-            y = placed([P, PACK, HALF], F32, "y" + name)
-            for r in range(PACK):
-                slots = slice(r * P, (r + 1) * P)
-                score = ps.tile([P, HALF], F32, name="score", bufs=6)
-                nc.tensor.matmul_mx(
-                    out=score[:],
-                    lhsT=k_codes[:, slots].bitcast(FP8X4),
-                    lhsT_scale=k_sc[:, slots],
-                    rhs=q_mx[0][:].bitcast(FP8X4),
-                    rhs_scale=q_mx[1][:],
-                    start=True,
-                    stop=True,
-                )
-                nc.vector.tensor_tensor(x[:, r, :], score[:], ls_all[:, cols], ALU.subtract)
-                nc.scalar.activation(y[:, r, :], x[:, r, :], ACT.Exp, bias=kb_col[:, r : r + 1])
-                if r % 2:
-                    nc.sync.dma_start(y_rows[:, r - 1 : r + 1, cols], y[:, r - 1 : r + 1, :])
+        def weigh(c):
+            x = placed([P, PACK, CHUNK], F32, "x%d" % c)
+            y = placed([P, PACK, CHUNK], F32, "y%d" % c)
+            for pair in range(2):
+                score = ps.tile([P, 2, CHUNK], F32, name="score", bufs=6)
+                for i in range(2):
+                    slots = slice((2 * pair + i) * P, (2 * pair + i + 1) * P)
+                    nc.tensor.matmul_mx(
+                        out=score[:, i, :],
+                        lhsT=k_codes[:, slots].bitcast(FP8X4),
+                        lhsT_scale=k_sc[:, slots],
+                        rhs=q_codes[:, columns(c)].bitcast(FP8X4),
+                        rhs_scale=q_sc[:, columns(c)],
+                        start=True,
+                        stop=True,
+                    )
+                ls_twice = ls_all[:, columns(c)].unsqueeze(1).to_broadcast([P, 2, CHUNK])
+                nc.vector.tensor_tensor(x[:, 2 * pair : 2 * pair + 2, :], score[:], ls_twice, ALU.subtract)
+                for r in range(2 * pair, 2 * pair + 2):
+                    nc.scalar.activation(y[:, r, :], x[:, r, :], ACT.Exp, bias=kb_col[:, r : r + 1])
+            nc.sync.dma_start(y_rows[:, :, columns(c)], y[:])
             return y
 
-        def quantise_weights(y_bf, cols):
+        def quantise_weights(c, y):
+            y_bf = placed([P, CHUNK, PACK], BF16, "y_bf%d" % c)
+            if c == CHUNKS - 1:
+                nc.scalar.activation(woven(y_bf[:]), by_rows(y[:]), ACT.Copy)
+            else:
+                nc.vector.tensor_copy(woven(y_bf[:]), by_rows(y[:]))
             nc.vector.quantize_mx(
-                out=y_codes[:, cols].bitcast(FP8X4), scales=y_sc[:, cols], in_=y_bf[:].rearrange("p q r -> p (q r)")
+                out=y_codes[:, columns(c)].bitcast(FP8X4),
+                scales=y_sc[:, columns(c)],
+                in_=y_bf[:].rearrange("p q r -> p (q r)"),
             )
-            nc.sync.dma_start(y_words[:, cols], y_codes[:, cols].bitcast(I32))
 
-        early, late = slice(0, HALF), slice(HALF, NQ)
-        q_early = quantise_queries([q_first[:]], "_early", AT_SCALES)
-        k_codes = placed([P, N], U32, "k_codes")
-        nc.vector.tensor_copy(
-            k_codes[:].rearrange("p (r s) -> p s r", r=PACK), word_pool[:].bitcast(U32).indirect(offsets[:])
-        )
-        kb_got = placed([P, N], F32, "kb_got", AT_WORDS)
-        nc.vector.tensor_copy(kb_got[:], kb_pool[:].indirect(offsets[:]))
-        kb_ps = ps.tile([P, PACK, P], F32, name="kb_ps")
-        for r in range(PACK):
-            nc.tensor.transpose(kb_ps[:, r, :], kb_got[:, r::PACK], ident[:])
-        kb_col = placed([P, PACK], F32, "kb_col", AT_LS)
-        nc.scalar.copy(kb_col[:], kb_ps[:, :, 0])
-        q_late = quantise_queries([q_rest[:, 0], q_rest[:, 1]], "_late", AT_KB, AT_LATE_BF)
-        y_early = weigh(q_early, early, "_early", AT_LATE_BF)
-        y_late = weigh(q_late, late, "_late")
-
-        early_bf = placed([P, HALF, PACK], BF16, "early_bf")
-        late_bf = placed([P, HALF, PACK], BF16, "late_bf")
-        nc.vector.tensor_copy(woven(early_bf[:]), by_rows(y_early[:]))
-        nc.vector.tensor_copy(woven(late_bf[:, 0:CHUNK, :]), by_rows(y_late[:, :, 0:CHUNK]))
-        nc.scalar.activation(woven(late_bf[:, CHUNK:, :]), by_rows(y_late[:, :, CHUNK:]), ACT.Copy)
-        quantise_weights(early_bf, early)
-        quantise_weights(late_bf, late)
-        for quad in range(4):
-            queue = nc.sync if quad == 3 else nc.scalar
-            queue.dma_start(
-                out_2[0, 4 * quad : 4 * quad + 4, :].bitcast(I32),
-                y_sc[32 * quad : 32 * quad + 4, :].bitcast(I32),
-            )
+        ys = [weigh(c) for c in range(CHUNKS)]
+        last = (CHUNKS - 1) * CHUNK
+        for c in range(CHUNKS):
+            quantise_weights(c, ys[c])
+            if c == CHUNKS - 2:
+                nc.sync.dma_start(y_words[:, 0:last], y_codes[:, 0:last].bitcast(I32))
+        nc.sync.dma_start(y_words[:, last:], y_codes[:, last:].bitcast(I32))
+        for r in range(4):
+            queue = nc.sync if r % 2 else nc.scalar
+            queue.dma_start(out_2[0, r:16:4, :].bitcast(I32), y_sc[r:P:32, :].bitcast(I32))

@@ -1,7 +1,6 @@
 from contextlib import ExitStack
 
 import concourse.mybir as mybir
-from concourse.masks import make_identity
 
 N, T, D, NQ = 512, 2048, 512, 512
 FLOPS = 2 * N * D * NQ
@@ -19,10 +18,11 @@ ALU = mybir.AluOpType
 
 P = 128
 PACK = 4
+HALF = 256
+LATE_ON_VECTOR = 128
 CHUNK = 128
-CHUNKS = NQ // CHUNK
 KB_ROW = P - 1
-AT_KB_GOT, AT_LS_ROWS = 0, 2048
+AT_KB_GOT, AT_LS_ROWS, AT_ZEROS, AT_LAST_RAW = 0, 2048, 4096, 4608
 
 
 def tile_attend_plw_kb_topk_kernel(tc, qT, k_words, k_scales, kb, ls, offs, out_0, out_1, out_2):
@@ -43,22 +43,28 @@ def tile_attend_plw_kb_topk_kernel(tc, qT, k_words, k_scales, kb, ls, offs, out_
         def by_rows(rows):
             return rows.rearrange("p t (c i) -> p c t i", i=4)
 
-        def columns(c):
-            return slice(c * CHUNK, (c + 1) * CHUNK)
+        early, late = slice(0, HALF), slice(HALF, NQ)
 
         scale_pool = placed([P, T], U8, "scale_pool")
         nc.vector.memset(scale_pool[:].bitcast(I32), 0)
+        zeros = placed([P, P], F32, "zeros", AT_ZEROS)
+        nc.vector.memset(zeros[:], 0.0)
         ident = placed([P, P], F32, "ident")
-        nc.vector.memset(ident[:], 0.0)
-        make_identity(nc, ident[:], nomemset=True)
+        nc.gpsimd.affine_select(
+            out=ident[:],
+            in_=zeros[:],
+            compare_op=ALU.not_equal,
+            fill=1.0,
+            base=0,
+            pattern=[[-1, P]],
+            channel_multiplier=1,
+        )
         kb_pool = placed([P, T], F32, "kb_pool")
         nc.vector.memset(kb_pool[0:KB_ROW, :], 0.0)
 
         offsets = sb.tile([P, N // 16], U16, name="offsets")
         nc.sync.dma_start(offsets[:], offs)
         nc.scalar.dma_start(kb_pool[KB_ROW:P, :], kb[0:1, :])
-        q_rows = qT[0].rearrange("(p t) q -> p t q", t=PACK)
-        q_raw = [placed([P, PACK, CHUNK], F32, "q_raw%d" % c) for c in range(CHUNKS)]
         ls_rows = placed([P, PACK], F32, "ls_rows", AT_LS_ROWS)
         nc.sync.dma_start(ls_rows[:], ls[0, 0].rearrange("(p j) -> p j", j=PACK))
         for r in range(4):
@@ -66,17 +72,16 @@ def tile_attend_plw_kb_topk_kernel(tc, qT, k_words, k_scales, kb, ls, offs, out_
             queue.dma_start(scale_pool[r:P:32, :].bitcast(I32), k_scales[0, r:16:4, :].bitcast(I32))
         word_pool = placed([P, T], I32, "word_pool")
         nc.sync.dma_start(word_pool[:], k_words[0].rearrange("p t r -> p (t r)").bitcast(I32))
-        for c in range(CHUNKS):
-            nc.sync.dma_start(q_raw[c][:], q_rows[:, :, columns(c)])
+        q_rows = qT[0].rearrange("(p t) q -> p t q", t=PACK)
+        q_raw = [placed([P, PACK, CHUNK], F32, "q_raw%d" % c) for c in range(NQ // CHUNK - 1)]
+        q_raw.append(placed([P, PACK, CHUNK], F32, "q_raw_last", AT_LAST_RAW))
+        for c, raw in enumerate(q_raw):
+            nc.sync.dma_start(raw[:], q_rows[:, :, c * CHUNK : (c + 1) * CHUNK])
 
         kb_got = placed([P, N], F32, "kb_got", AT_KB_GOT)
         nc.vector.tensor_copy(kb_got[:], kb_pool[:].indirect(offsets[:]))
         scale_got = placed([P, N], U8, "scale_got")
         nc.vector.tensor_copy(scale_got[:], scale_pool[:].indirect(offsets[:]))
-        k_sc = placed([P, N], U8, "k_sc")
-        nc.vector.tensor_copy(
-            k_sc[:].rearrange("p (r s) -> p r s", r=PACK), scale_got[:].rearrange("p (s r) -> p r s", r=PACK)
-        )
 
         ls_ps = ps.tile([P, PACK, P], F32, name="ls_ps")
         for j in range(PACK):
@@ -95,16 +100,21 @@ def tile_attend_plw_kb_topk_kernel(tc, qT, k_words, k_scales, kb, ls, offs, out_
         nc.vector.tensor_copy(
             k_codes[:].rearrange("p (r s) -> p s r", r=PACK), word_pool[:].bitcast(U32).indirect(offsets[:])
         )
+        k_sc = placed([P, N], U8, "k_sc", AT_ZEROS)
+        nc.vector.tensor_copy(
+            k_sc[:].rearrange("p (r s) -> p r s", r=PACK), scale_got[:].rearrange("p (s r) -> p r s", r=PACK)
+        )
 
         q_bf = placed([P, NQ, PACK], BF16, "q_bf", AT_KB_GOT)
         q_codes = placed([P, NQ], U32, "q_codes")
         q_sc = placed([P, NQ], U8, "q_sc")
-        for c in range(CHUNKS):
-            nc.scalar.activation(woven(q_bf[:, columns(c), :]), by_rows(q_raw[c][:]), ACT.Copy)
+        for c, raw in enumerate(q_raw):
+            nc.scalar.activation(woven(q_bf[:, c * CHUNK : (c + 1) * CHUNK, :]), by_rows(raw[:]), ACT.Copy)
+        for cols in (early, late):
             nc.vector.quantize_mx(
-                out=q_codes[:, columns(c)].bitcast(FP8X4),
-                scales=q_sc[:, columns(c)],
-                in_=q_bf[:, columns(c), :].rearrange("p q t -> p (q t)"),
+                out=q_codes[:, cols].bitcast(FP8X4),
+                scales=q_sc[:, cols],
+                in_=q_bf[:, cols, :].rearrange("p q t -> p (q t)"),
             )
 
         y_rows = out_0.rearrange("(p r) q -> p r q", r=PACK)
@@ -112,48 +122,43 @@ def tile_attend_plw_kb_topk_kernel(tc, qT, k_words, k_scales, kb, ls, offs, out_
         y_codes = placed([P, NQ], U32, "y_codes")
         y_sc = placed([P, NQ], U8, "y_sc")
 
-        def weigh(c):
-            x = placed([P, PACK, CHUNK], F32, "x%d" % c)
-            y = placed([P, PACK, CHUNK], F32, "y%d" % c)
-            for pair in range(2):
-                score = ps.tile([P, 2, CHUNK], F32, name="score", bufs=6)
-                for i in range(2):
-                    slots = slice((2 * pair + i) * P, (2 * pair + i + 1) * P)
-                    nc.tensor.matmul_mx(
-                        out=score[:, i, :],
-                        lhsT=k_codes[:, slots].bitcast(FP8X4),
-                        lhsT_scale=k_sc[:, slots],
-                        rhs=q_codes[:, columns(c)].bitcast(FP8X4),
-                        rhs_scale=q_sc[:, columns(c)],
-                        start=True,
-                        stop=True,
-                    )
-                ls_twice = ls_all[:, columns(c)].unsqueeze(1).to_broadcast([P, 2, CHUNK])
-                nc.vector.tensor_tensor(x[:, 2 * pair : 2 * pair + 2, :], score[:], ls_twice, ALU.subtract)
-                for r in range(2 * pair, 2 * pair + 2):
-                    nc.scalar.activation(y[:, r, :], x[:, r, :], ACT.Exp, bias=kb_col[:, r : r + 1])
-            nc.sync.dma_start(y_rows[:, :, columns(c)], y[:])
+        def weigh(cols, name, at_x=None):
+            x = placed([P, PACK, HALF], F32, "x" + name, at_x)
+            y = placed([P, PACK, HALF], F32, "y" + name)
+            for r in range(PACK):
+                slots = slice(r * P, (r + 1) * P)
+                score = ps.tile([P, HALF], F32, name="score", bufs=6)
+                nc.tensor.matmul_mx(
+                    out=score[:],
+                    lhsT=k_codes[:, slots].bitcast(FP8X4),
+                    lhsT_scale=k_sc[:, slots],
+                    rhs=q_codes[:, cols].bitcast(FP8X4),
+                    rhs_scale=q_sc[:, cols],
+                    start=True,
+                    stop=True,
+                )
+                nc.vector.tensor_tensor(x[:, r, :], score[:], ls_all[:, cols], ALU.subtract)
+                nc.scalar.activation(y[:, r, :], x[:, r, :], ACT.Exp, bias=kb_col[:, r : r + 1])
+                if r % 2:
+                    nc.sync.dma_start(y_rows[:, r - 1 : r + 1, cols], y[:, r - 1 : r + 1, :])
             return y
 
-        def quantise_weights(c, y):
-            y_bf = placed([P, CHUNK, PACK], BF16, "y_bf%d" % c)
-            if c == CHUNKS - 1:
-                nc.scalar.activation(woven(y_bf[:]), by_rows(y[:]), ACT.Copy)
-            else:
-                nc.vector.tensor_copy(woven(y_bf[:]), by_rows(y[:]))
+        def quantise_weights(y_bf, cols):
             nc.vector.quantize_mx(
-                out=y_codes[:, columns(c)].bitcast(FP8X4),
-                scales=y_sc[:, columns(c)],
-                in_=y_bf[:].rearrange("p q r -> p (q r)"),
+                out=y_codes[:, cols].bitcast(FP8X4), scales=y_sc[:, cols], in_=y_bf[:].rearrange("p q r -> p (q r)")
             )
+            nc.sync.dma_start(y_words[:, cols], y_codes[:, cols].bitcast(I32))
 
-        ys = [weigh(c) for c in range(CHUNKS)]
-        last = (CHUNKS - 1) * CHUNK
-        for c in range(CHUNKS):
-            quantise_weights(c, ys[c])
-            if c == CHUNKS - 2:
-                nc.sync.dma_start(y_words[:, 0:last], y_codes[:, 0:last].bitcast(I32))
-        nc.sync.dma_start(y_words[:, last:], y_codes[:, last:].bitcast(I32))
+        y_early = weigh(early, "_early", AT_LAST_RAW)
+        y_late = weigh(late, "_late")
+
+        early_bf = placed([P, HALF, PACK], BF16, "early_bf")
+        late_bf = placed([P, HALF, PACK], BF16, "late_bf")
+        nc.vector.tensor_copy(woven(early_bf[:]), by_rows(y_early[:]))
+        nc.vector.tensor_copy(woven(late_bf[:, 0:LATE_ON_VECTOR, :]), by_rows(y_late[:, :, 0:LATE_ON_VECTOR]))
+        nc.scalar.activation(woven(late_bf[:, LATE_ON_VECTOR:, :]), by_rows(y_late[:, :, LATE_ON_VECTOR:]), ACT.Copy)
+        quantise_weights(early_bf, early)
+        quantise_weights(late_bf, late)
         for r in range(4):
             queue = nc.sync if r % 2 else nc.scalar
             queue.dma_start(out_2[0, r:16:4, :].bitcast(I32), y_sc[r:P:32, :].bitcast(I32))

@@ -19,10 +19,9 @@ ALU = mybir.AluOpType
 P = 128
 PACK = 4
 HALF = 256
-LATE_ON_VECTOR = 128
 CHUNK = 128
 KB_ROW = P - 1
-AT_KB_GOT, AT_LS_ROWS, AT_ZEROS, AT_LAST_RAW = 0, 2048, 4096, 4608
+AT_KB_GOT, AT_LS_ROWS, AT_ZEROS, AT_THIRD_RAW = 0, 2048, 4096, 4608
 
 
 def tile_attend_plw_kb_topk_kernel(tc, qT, k_words, k_scales, kb, ls, offs, out_0, out_1, out_2):
@@ -43,7 +42,8 @@ def tile_attend_plw_kb_topk_kernel(tc, qT, k_words, k_scales, kb, ls, offs, out_
         def by_rows(rows):
             return rows.rearrange("p t (c i) -> p c t i", i=4)
 
-        early, late = slice(0, HALF), slice(HALF, NQ)
+        first, middle, last = slice(0, CHUNK), slice(CHUNK, NQ - CHUNK), slice(NQ - CHUNK, NQ)
+        parts = (first, middle, last)
 
         scale_pool = placed([P, T], U8, "scale_pool")
         nc.vector.memset(scale_pool[:].bitcast(I32), 0)
@@ -73,8 +73,9 @@ def tile_attend_plw_kb_topk_kernel(tc, qT, k_words, k_scales, kb, ls, offs, out_
         word_pool = placed([P, T], I32, "word_pool")
         nc.sync.dma_start(word_pool[:], k_words[0].rearrange("p t r -> p (t r)").bitcast(I32))
         q_rows = qT[0].rearrange("(p t) q -> p t q", t=PACK)
-        q_raw = [placed([P, PACK, CHUNK], F32, "q_raw%d" % c) for c in range(NQ // CHUNK - 1)]
-        q_raw.append(placed([P, PACK, CHUNK], F32, "q_raw_last", AT_LAST_RAW))
+        q_raw = [
+            placed([P, PACK, CHUNK], F32, "q_raw%d" % c, AT_THIRD_RAW if c == 2 else None) for c in range(NQ // CHUNK)
+        ]
         for c, raw in enumerate(q_raw):
             nc.sync.dma_start(raw[:], q_rows[:, :, c * CHUNK : (c + 1) * CHUNK])
 
@@ -110,7 +111,7 @@ def tile_attend_plw_kb_topk_kernel(tc, qT, k_words, k_scales, kb, ls, offs, out_
         q_sc = placed([P, NQ], U8, "q_sc")
         for c, raw in enumerate(q_raw):
             nc.scalar.activation(woven(q_bf[:, c * CHUNK : (c + 1) * CHUNK, :]), by_rows(raw[:]), ACT.Copy)
-        for cols in (early, late):
+        for cols in parts:
             nc.vector.quantize_mx(
                 out=q_codes[:, cols].bitcast(FP8X4),
                 scales=q_sc[:, cols],
@@ -123,42 +124,51 @@ def tile_attend_plw_kb_topk_kernel(tc, qT, k_words, k_scales, kb, ls, offs, out_
         y_sc = placed([P, NQ], U8, "y_sc")
 
         def weigh(cols, name, at_x=None):
-            x = placed([P, PACK, HALF], F32, "x" + name, at_x)
-            y = placed([P, PACK, HALF], F32, "y" + name)
-            for r in range(PACK):
-                slots = slice(r * P, (r + 1) * P)
-                score = ps.tile([P, HALF], F32, name="score", bufs=6)
-                nc.tensor.matmul_mx(
-                    out=score[:],
-                    lhsT=k_codes[:, slots].bitcast(FP8X4),
-                    lhsT_scale=k_sc[:, slots],
-                    rhs=q_codes[:, cols].bitcast(FP8X4),
-                    rhs_scale=q_sc[:, cols],
-                    start=True,
-                    stop=True,
-                )
-                nc.vector.tensor_tensor(x[:, r, :], score[:], ls_all[:, cols], ALU.subtract)
-                nc.scalar.activation(y[:, r, :], x[:, r, :], ACT.Exp, bias=kb_col[:, r : r + 1])
-                if r % 2:
-                    nc.sync.dma_start(y_rows[:, r - 1 : r + 1, cols], y[:, r - 1 : r + 1, :])
+            width = cols.stop - cols.start
+            together = HALF // width
+            y = placed([P, PACK, width], F32, "y" + name)
+            for r0 in range(0, PACK, together):
+                score = ps.tile([P, together, width], F32, name="score", bufs=6)
+                for i in range(together):
+                    slots = slice((r0 + i) * P, (r0 + i + 1) * P)
+                    nc.tensor.matmul_mx(
+                        out=score[:, i, :],
+                        lhsT=k_codes[:, slots].bitcast(FP8X4),
+                        lhsT_scale=k_sc[:, slots],
+                        rhs=q_codes[:, cols].bitcast(FP8X4),
+                        rhs_scale=q_sc[:, cols],
+                        start=True,
+                        stop=True,
+                    )
+                x = placed([P, together, width], F32, "x%s%d" % (name, r0), at_x and at_x + 4 * r0 * width)
+                ls_here = ls_all[:, cols].unsqueeze(1).to_broadcast([P, together, width])
+                nc.vector.tensor_tensor(x[:], score[:], ls_here, ALU.subtract)
+                for i in range(together):
+                    r = r0 + i
+                    nc.scalar.activation(y[:, r, :], x[:, i, :], ACT.Exp, bias=kb_col[:, r : r + 1])
+                done = r0 + together
+                rows = 2 * together
+                if done % rows == 0:
+                    nc.sync.dma_start(y_rows[:, done - rows : done, cols], y[:, done - rows : done, :])
             return y
 
         def quantise_weights(y_bf, cols):
             nc.vector.quantize_mx(
                 out=y_codes[:, cols].bitcast(FP8X4), scales=y_sc[:, cols], in_=y_bf[:].rearrange("p q r -> p (q r)")
             )
-            nc.sync.dma_start(y_words[:, cols], y_codes[:, cols].bitcast(I32))
 
-        y_early = weigh(early, "_early", AT_LAST_RAW)
-        y_late = weigh(late, "_late")
-
-        early_bf = placed([P, HALF, PACK], BF16, "early_bf")
-        late_bf = placed([P, HALF, PACK], BF16, "late_bf")
-        nc.vector.tensor_copy(woven(early_bf[:]), by_rows(y_early[:]))
-        nc.vector.tensor_copy(woven(late_bf[:, 0:LATE_ON_VECTOR, :]), by_rows(y_late[:, :, 0:LATE_ON_VECTOR]))
-        nc.scalar.activation(woven(late_bf[:, LATE_ON_VECTOR:, :]), by_rows(y_late[:, :, LATE_ON_VECTOR:]), ACT.Copy)
-        quantise_weights(early_bf, early)
-        quantise_weights(late_bf, late)
+        y_first, y_middle, y_last = weigh(first, "_first", AT_THIRD_RAW), weigh(middle, "_middle"), weigh(last, "_last")
+        first_bf = placed([P, CHUNK, PACK], BF16, "first_bf")
+        middle_bf = placed([P, HALF, PACK], BF16, "middle_bf")
+        last_bf = placed([P, CHUNK, PACK], BF16, "last_bf")
+        nc.vector.tensor_copy(woven(first_bf[:]), by_rows(y_first[:]))
+        nc.vector.tensor_copy(woven(middle_bf[:]), by_rows(y_middle[:]))
+        nc.scalar.activation(woven(last_bf[:]), by_rows(y_last[:]), ACT.Copy)
+        quantise_weights(first_bf, first)
+        quantise_weights(middle_bf, middle)
+        nc.sync.dma_start(y_words[:, 0 : last.start], y_codes[:, 0 : last.start].bitcast(I32))
+        quantise_weights(last_bf, last)
+        nc.sync.dma_start(y_words[:, last], y_codes[:, last].bitcast(I32))
         for r in range(4):
             queue = nc.sync if r % 2 else nc.scalar
             queue.dma_start(out_2[0, r:16:4, :].bitcast(I32), y_sc[r:P:32, :].bitcast(I32))

@@ -20,6 +20,7 @@ P = 128
 PACK = 4
 HALF = 256
 CHUNK = 128
+LAST_ON_VECTOR = 80
 KB_ROW = P - 1
 AT_KB_GOT, AT_LS_ROWS, AT_ZEROS, AT_THIRD_RAW = 0, 2048, 4096, 4608
 
@@ -161,9 +162,10 @@ def tile_attend_plw_kb_topk_kernel(tc, qT, k_words, k_scales, kb, ls, offs, out_
         first_bf = placed([P, CHUNK, PACK], BF16, "first_bf")
         middle_bf = placed([P, HALF, PACK], BF16, "middle_bf")
         last_bf = placed([P, CHUNK, PACK], BF16, "last_bf")
-        nc.vector.tensor_copy(woven(first_bf[:]), by_rows(y_first[:]))
+        nc.gpsimd.tensor_scalar(first_bf[:], y_first[:].rearrange("p r q -> p q r"), 1.0, 0.0, ALU.mult, ALU.add)
         nc.vector.tensor_copy(woven(middle_bf[:]), by_rows(y_middle[:]))
-        nc.scalar.activation(woven(last_bf[:]), by_rows(y_last[:]), ACT.Copy)
+        nc.vector.tensor_copy(woven(last_bf[:, 0:LAST_ON_VECTOR, :]), by_rows(y_last[:, :, 0:LAST_ON_VECTOR]))
+        nc.scalar.activation(woven(last_bf[:, LAST_ON_VECTOR:, :]), by_rows(y_last[:, :, LAST_ON_VECTOR:]), ACT.Copy)
         quantise_weights(first_bf, first)
         quantise_weights(middle_bf, middle)
         nc.sync.dma_start(y_words[:, 0 : last.start], y_codes[:, 0 : last.start].bitcast(I32))

@@ -124,7 +124,7 @@ def tile_attend_plw_kb_topk_kernel(tc, qT, k_words, k_scales, kb, ls, offs, out_
         y_codes = placed([P, NQ], U32, "y_codes")
         y_sc = placed([P, NQ], U8, "y_sc")
 
-        def weigh(cols, name, at_x=None):
+        def weigh(cols, name, rows, at_x=None):
             width = cols.stop - cols.start
             together = HALF // width
             y = placed([P, PACK, width], F32, "y" + name)
@@ -148,7 +148,6 @@ def tile_attend_plw_kb_topk_kernel(tc, qT, k_words, k_scales, kb, ls, offs, out_
                     r = r0 + i
                     nc.scalar.activation(y[:, r, :], x[:, i, :], ACT.Exp, bias=kb_col[:, r : r + 1])
                 done = r0 + together
-                rows = 2 * together
                 if done % rows == 0:
                     nc.sync.dma_start(y_rows[:, done - rows : done, cols], y[:, done - rows : done, :])
             return y
@@ -158,7 +157,7 @@ def tile_attend_plw_kb_topk_kernel(tc, qT, k_words, k_scales, kb, ls, offs, out_
                 out=y_codes[:, cols].bitcast(FP8X4), scales=y_sc[:, cols], in_=y_bf[:].rearrange("p q r -> p (q r)")
             )
 
-        y_first, y_middle, y_last = weigh(first, "_first", AT_THIRD_RAW), weigh(middle, "_middle"), weigh(last, "_last")
+        y_first, y_middle, y_last = weigh(first, "_first", 2, AT_THIRD_RAW), weigh(middle, "_middle", 2), weigh(last, "_last", 4)
         first_bf = placed([P, CHUNK, PACK], BF16, "first_bf")
         middle_bf = placed([P, HALF, PACK], BF16, "middle_bf")
         last_bf = placed([P, CHUNK, PACK], BF16, "last_bf")

@@ -22,7 +22,8 @@ HALF = 256
 CHUNK = 128
 LAST_ON_VECTOR = 80
 KB_ROW = P - 1
-AT_KB_GOT, AT_LS_ROWS, AT_ZEROS, AT_THIRD_RAW = 0, 2048, 4096, 4608
+AT_KB_GOT, AT_LS_ROWS, AT_ZEROS, AT_THIRD_RAW, AT_FIRST_RAW = 0, 2048, 4096, 4608, 6656
+AT_RAW = (AT_FIRST_RAW, None, AT_THIRD_RAW, None)
 
 
 def tile_attend_plw_kb_topk_kernel(tc, qT, k_words, k_scales, kb, ls, offs, out_0, out_1, out_2):
@@ -44,7 +45,6 @@ def tile_attend_plw_kb_topk_kernel(tc, qT, k_words, k_scales, kb, ls, offs, out_
             return rows.rearrange("p t (c i) -> p c t i", i=4)
 
         first, middle, last = slice(0, CHUNK), slice(CHUNK, NQ - CHUNK), slice(NQ - CHUNK, NQ)
-        parts = (first, middle, last)
 
         scale_pool = placed([P, T], U8, "scale_pool")
         nc.vector.memset(scale_pool[:].bitcast(I32), 0)
@@ -75,7 +75,7 @@ def tile_attend_plw_kb_topk_kernel(tc, qT, k_words, k_scales, kb, ls, offs, out_
         nc.sync.dma_start(word_pool[:], k_words[0].rearrange("p t r -> p (t r)").bitcast(I32))
         q_rows = qT[0].rearrange("(p t) q -> p t q", t=PACK)
         q_raw = [
-            placed([P, PACK, CHUNK], F32, "q_raw%d" % c, AT_THIRD_RAW if c == 2 else None) for c in range(NQ // CHUNK)
+            placed([P, PACK, CHUNK], F32, "q_raw%d" % c, AT_RAW[c]) for c in range(NQ // CHUNK)
         ]
         for c, raw in enumerate(q_raw):
             nc.sync.dma_start(raw[:], q_rows[:, :, c * CHUNK : (c + 1) * CHUNK])
@@ -102,29 +102,38 @@ def tile_attend_plw_kb_topk_kernel(tc, qT, k_words, k_scales, kb, ls, offs, out_
         nc.vector.tensor_copy(
             k_codes[:].rearrange("p (r s) -> p s r", r=PACK), word_pool[:].bitcast(U32).indirect(offsets[:])
         )
-        k_sc = placed([P, N], U8, "k_sc", AT_ZEROS)
-        nc.vector.tensor_copy(
-            k_sc[:].rearrange("p (r s) -> p r s", r=PACK), scale_got[:].rearrange("p (s r) -> p r s", r=PACK)
-        )
 
+        def deal_scales(pair, at):
+            dealt = placed([P, 2, P], U8, "k_sc%d" % pair, at)
+            by_place = scale_got[:].rearrange("p (s r) -> p r s", r=PACK)
+            nc.vector.tensor_copy(dealt[:], by_place[:, 2 * pair : 2 * pair + 2, :])
+            return [dealt[:, 0, :], dealt[:, 1, :]]
+
+        k_sc = deal_scales(0, AT_ZEROS)
         q_bf = placed([P, NQ, PACK], BF16, "q_bf", AT_KB_GOT)
         q_codes = placed([P, NQ], U32, "q_codes")
         q_sc = placed([P, NQ], U8, "q_sc")
         for c, raw in enumerate(q_raw):
             nc.scalar.activation(woven(q_bf[:, c * CHUNK : (c + 1) * CHUNK, :]), by_rows(raw[:]), ACT.Copy)
-        for cols in parts:
+
+        def quantise_queries(cols):
             nc.vector.quantize_mx(
                 out=q_codes[:, cols].bitcast(FP8X4),
                 scales=q_sc[:, cols],
                 in_=q_bf[:, cols, :].rearrange("p q t -> p (q t)"),
             )
 
+        quantise_queries(first)
+        k_sc = k_sc + deal_scales(1, AT_FIRST_RAW)
+        quantise_queries(middle)
+        quantise_queries(last)
+
         y_rows = out_0.rearrange("(p r) q -> p r q", r=PACK)
         y_words = out_1[0].rearrange("p q u -> p (q u)").bitcast(I32)
         y_codes = placed([P, NQ], U32, "y_codes")
         y_sc = placed([P, NQ], U8, "y_sc")
 
-        def weigh(cols, name, rows, at_x=None):
+        def weigh(cols, name, store_at, at_x=None):
             width = cols.stop - cols.start
             together = HALF // width
             y = placed([P, PACK, width], F32, "y" + name)
@@ -135,7 +144,7 @@ def tile_attend_plw_kb_topk_kernel(tc, qT, k_words, k_scales, kb, ls, offs, out_
                     nc.tensor.matmul_mx(
                         out=score[:, i, :],
                         lhsT=k_codes[:, slots].bitcast(FP8X4),
-                        lhsT_scale=k_sc[:, slots],
+                        lhsT_scale=k_sc[r0 + i],
                         rhs=q_codes[:, cols].bitcast(FP8X4),
                         rhs_scale=q_sc[:, cols],
                         start=True,
@@ -148,8 +157,9 @@ def tile_attend_plw_kb_topk_kernel(tc, qT, k_words, k_scales, kb, ls, offs, out_
                     r = r0 + i
                     nc.scalar.activation(y[:, r, :], x[:, i, :], ACT.Exp, bias=kb_col[:, r : r + 1])
                 done = r0 + together
-                if done % rows == 0:
-                    nc.sync.dma_start(y_rows[:, done - rows : done, cols], y[:, done - rows : done, :])
+                if done in store_at:
+                    rows = slice(store_at[store_at.index(done) - 1], done)
+                    nc.sync.dma_start(y_rows[:, rows, cols], y[:, rows, :])
             return y
 
         def quantise_weights(y_bf, cols):
@@ -157,7 +167,9 @@ def tile_attend_plw_kb_topk_kernel(tc, qT, k_words, k_scales, kb, ls, offs, out_
                 out=y_codes[:, cols].bitcast(FP8X4), scales=y_sc[:, cols], in_=y_bf[:].rearrange("p q r -> p (q r)")
             )
 
-        y_first, y_middle, y_last = weigh(first, "_first", 2, AT_THIRD_RAW), weigh(middle, "_middle", 2), weigh(last, "_last", 4)
+        y_first = weigh(first, "_first", (0, 2, 4), AT_THIRD_RAW)
+        y_middle = weigh(middle, "_middle", (0, 1, 2, 4))
+        y_last = weigh(last, "_last", (0, 4))
         first_bf = placed([P, CHUNK, PACK], BF16, "first_bf")
         middle_bf = placed([P, HALF, PACK], BF16, "middle_bf")
         last_bf = placed([P, CHUNK, PACK], BF16, "last_bf")

@@ -22,8 +22,8 @@ HALF = 256
 CHUNK = 128
 LAST_ON_VECTOR = 80
 KB_ROW = P - 1
-AT_KB_GOT, AT_LS_ROWS, AT_ZEROS, AT_THIRD_RAW, AT_FIRST_RAW = 0, 2048, 4096, 4608, 6656
-AT_RAW = (AT_FIRST_RAW, None, AT_THIRD_RAW, None)
+AT_KB_GOT, AT_LS_ROWS, AT_K_SC, AT_ZEROS, AT_K_CODES, AT_THIRD_RAW = 0, 2048, 4096, 4544, 4608, 6656
+AT_RAW = (None, None, AT_THIRD_RAW, None)
 
 
 def tile_attend_plw_kb_topk_kernel(tc, qT, k_words, k_scales, kb, ls, offs, out_0, out_1, out_2):
@@ -98,18 +98,14 @@ def tile_attend_plw_kb_topk_kernel(tc, qT, k_words, k_scales, kb, ls, offs, out_
         kb_col = placed([P, PACK], F32, "kb_col")
         nc.scalar.copy(kb_col[:], kb_ps[:, :, KB_ROW])
 
-        k_codes = placed([P, N], U32, "k_codes")
+        dealt = placed([P, PACK, P], U8, "k_sc", AT_K_SC)
+        nc.vector.tensor_copy(dealt[:], scale_got[:].rearrange("p (s r) -> p r s", r=PACK))
+        k_sc = [dealt[:, r, :] for r in range(PACK)]
+        k_codes = placed([P, N], U32, "k_codes", AT_K_CODES)
         nc.vector.tensor_copy(
             k_codes[:].rearrange("p (r s) -> p s r", r=PACK), word_pool[:].bitcast(U32).indirect(offsets[:])
         )
 
-        def deal_scales(pair, at):
-            dealt = placed([P, 2, P], U8, "k_sc%d" % pair, at)
-            by_place = scale_got[:].rearrange("p (s r) -> p r s", r=PACK)
-            nc.vector.tensor_copy(dealt[:], by_place[:, 2 * pair : 2 * pair + 2, :])
-            return [dealt[:, 0, :], dealt[:, 1, :]]
-
-        k_sc = deal_scales(0, AT_ZEROS)
         q_bf = placed([P, NQ, PACK], BF16, "q_bf", AT_KB_GOT)
         q_codes = placed([P, NQ], U32, "q_codes")
         q_sc = placed([P, NQ], U8, "q_sc")
@@ -124,7 +120,6 @@ def tile_attend_plw_kb_topk_kernel(tc, qT, k_words, k_scales, kb, ls, offs, out_
             )
 
         quantise_queries(first)
-        k_sc = k_sc + deal_scales(1, AT_FIRST_RAW)
         quantise_queries(middle)
         quantise_queries(last)
 

@@ -18,12 +18,15 @@ ALU = mybir.AluOpType
 
 P = 128
 PACK = 4
-HALF = 256
 CHUNK = 128
+CHUNKS = NQ // CHUNK
 LAST_ON_VECTOR = 80
 KB_ROW = P - 1
-AT_KB_GOT, AT_LS_ROWS, AT_K_SC, AT_ZEROS, AT_K_CODES, AT_THIRD_RAW = 0, 2048, 4096, 4544, 4608, 6656
-AT_RAW = (None, None, AT_THIRD_RAW, None)
+KEYS_AHEAD = 768
+AT_LS_ROWS = 960
+AT_RAW = (2048, 8192, 4096, None)
+AT_Q_BF = (0, AT_RAW[0], 1024, AT_RAW[2])
+AT_Q_SC = (6144, 6272, 6144, 6272)
 
 
 def tile_attend_plw_kb_topk_kernel(tc, qT, k_words, k_scales, kb, ls, offs, out_0, out_1, out_2):
@@ -44,11 +47,12 @@ def tile_attend_plw_kb_topk_kernel(tc, qT, k_words, k_scales, kb, ls, offs, out_
         def by_rows(rows):
             return rows.rearrange("p t (c i) -> p c t i", i=4)
 
-        first, middle, last = slice(0, CHUNK), slice(CHUNK, NQ - CHUNK), slice(NQ - CHUNK, NQ)
+        def columns(c):
+            return slice(c * CHUNK, (c + 1) * CHUNK)
 
         scale_pool = placed([P, T], U8, "scale_pool")
         nc.vector.memset(scale_pool[:].bitcast(I32), 0)
-        zeros = placed([P, P], F32, "zeros", AT_ZEROS)
+        zeros = placed([P, P], F32, "zeros")
         nc.vector.memset(zeros[:], 0.0)
         ident = placed([P, P], F32, "ident")
         nc.gpsimd.affine_select(
@@ -63,27 +67,47 @@ def tile_attend_plw_kb_topk_kernel(tc, qT, k_words, k_scales, kb, ls, offs, out_
         kb_pool = placed([P, T], F32, "kb_pool")
         nc.vector.memset(kb_pool[0:KB_ROW, :], 0.0)
 
+        q_rows = qT[0].rearrange("(p t) q -> p t q", t=PACK)
+        q_raw = [placed([P, PACK, CHUNK], F32, "q_raw%d" % c, AT_RAW[c]) for c in range(CHUNKS)]
         offsets = sb.tile([P, N // 16], U16, name="offsets")
         nc.sync.dma_start(offsets[:], offs)
         nc.scalar.dma_start(kb_pool[KB_ROW:P, :], kb[0:1, :])
-        ls_rows = placed([P, PACK], F32, "ls_rows", AT_LS_ROWS)
-        nc.sync.dma_start(ls_rows[:], ls[0, 0].rearrange("(p j) -> p j", j=PACK))
+        word_pool = placed([P, T], I32, "word_pool")
+        words = k_words[0].rearrange("p t r -> p (t r)").bitcast(I32)
+        nc.sync.dma_start(word_pool[:, 0:KEYS_AHEAD], words[:, 0:KEYS_AHEAD])
+        ls_rows = placed([P, 32], F32, "ls_rows", AT_LS_ROWS)
+        nc.sync.dma_start(ls_rows[:, 0:PACK], ls[0, 0].rearrange("(p j) -> p j", j=PACK))
         for r in range(4):
             queue = nc.scalar if r % 2 else nc.sync
             queue.dma_start(scale_pool[r:P:32, :].bitcast(I32), k_scales[0, r:16:4, :].bitcast(I32))
-        word_pool = placed([P, T], I32, "word_pool")
-        nc.sync.dma_start(word_pool[:], k_words[0].rearrange("p t r -> p (t r)").bitcast(I32))
-        q_rows = qT[0].rearrange("(p t) q -> p t q", t=PACK)
-        q_raw = [
-            placed([P, PACK, CHUNK], F32, "q_raw%d" % c, AT_RAW[c]) for c in range(NQ // CHUNK)
-        ]
-        for c, raw in enumerate(q_raw):
-            nc.sync.dma_start(raw[:], q_rows[:, :, c * CHUNK : (c + 1) * CHUNK])
+        nc.sync.dma_start(word_pool[:, KEYS_AHEAD:], words[:, KEYS_AHEAD:])
+        for c in range(CHUNKS):
+            nc.sync.dma_start(q_raw[c][:], q_rows[:, :, columns(c)])
 
-        kb_got = placed([P, N], F32, "kb_got", AT_KB_GOT)
+        kb_got = placed([P, N], F32, "kb_got")
         nc.vector.tensor_copy(kb_got[:], kb_pool[:].indirect(offsets[:]))
         scale_got = placed([P, N], U8, "scale_got")
         nc.vector.tensor_copy(scale_got[:], scale_pool[:].indirect(offsets[:]))
+
+        q_codes = placed([P, NQ], U32, "q_codes")
+        q_sc = [placed([P, CHUNK], U8, "q_sc%d" % c, AT_Q_SC[c]) for c in range(CHUNKS)]
+        q_bf = [placed([P, CHUNK, PACK], BF16, "q_bf%d" % c, AT_Q_BF[c])[:] for c in range(CHUNKS)]
+
+        def weave_on_scalar(words_bf, rows):
+            nc.scalar.activation(woven(words_bf), by_rows(rows), ACT.Copy)
+
+        def weave_on_vector(words_bf, rows):
+            nc.vector.tensor_copy(woven(words_bf), by_rows(rows))
+
+        def weave_on_gpsimd(words_bf, rows):
+            nc.gpsimd.tensor_scalar(words_bf, rows.rearrange("p r q -> p q r"), 1.0, 0.0, ALU.mult, ALU.add)
+
+        def quantise(codes, scales, words_bf, c):
+            nc.vector.quantize_mx(
+                out=codes[:, columns(c)].bitcast(FP8X4),
+                scales=scales,
+                in_=words_bf.rearrange("p q t -> p (q t)"),
+            )
 
         ls_ps = ps.tile([P, PACK, P], F32, name="ls_ps")
         for j in range(PACK):
@@ -98,85 +122,74 @@ def tile_attend_plw_kb_topk_kernel(tc, qT, k_words, k_scales, kb, ls, offs, out_
         kb_col = placed([P, PACK], F32, "kb_col")
         nc.scalar.copy(kb_col[:], kb_ps[:, :, KB_ROW])
 
-        dealt = placed([P, PACK, P], U8, "k_sc", AT_K_SC)
-        nc.vector.tensor_copy(dealt[:], scale_got[:].rearrange("p (s r) -> p r s", r=PACK))
-        k_sc = [dealt[:, r, :] for r in range(PACK)]
-        k_codes = placed([P, N], U32, "k_codes", AT_K_CODES)
+        k_sc = placed([P, PACK, P], U8, "k_sc")
+        nc.vector.tensor_copy(k_sc[:], scale_got[:].rearrange("p (s r) -> p r s", r=PACK))
+        k_codes = placed([P, N], U32, "k_codes")
         nc.vector.tensor_copy(
             k_codes[:].rearrange("p (r s) -> p s r", r=PACK), word_pool[:].bitcast(U32).indirect(offsets[:])
         )
-
-        q_bf = placed([P, NQ, PACK], BF16, "q_bf", AT_KB_GOT)
-        q_codes = placed([P, NQ], U32, "q_codes")
-        q_sc = placed([P, NQ], U8, "q_sc")
-        for c, raw in enumerate(q_raw):
-            nc.scalar.activation(woven(q_bf[:, c * CHUNK : (c + 1) * CHUNK, :]), by_rows(raw[:]), ACT.Copy)
-
-        def quantise_queries(cols):
-            nc.vector.quantize_mx(
-                out=q_codes[:, cols].bitcast(FP8X4),
-                scales=q_sc[:, cols],
-                in_=q_bf[:, cols, :].rearrange("p q t -> p (q t)"),
-            )
-
-        quantise_queries(first)
-        quantise_queries(middle)
-        quantise_queries(last)
 
         y_rows = out_0.rearrange("(p r) q -> p r q", r=PACK)
         y_words = out_1[0].rearrange("p q u -> p (q u)").bitcast(I32)
         y_codes = placed([P, NQ], U32, "y_codes")
         y_sc = placed([P, NQ], U8, "y_sc")
 
-        def weigh(cols, name, store_at, at_x=None):
-            width = cols.stop - cols.start
-            together = HALF // width
-            y = placed([P, PACK, width], F32, "y" + name)
-            for r0 in range(0, PACK, together):
-                score = ps.tile([P, together, width], F32, name="score", bufs=6)
-                for i in range(together):
-                    slots = slice((r0 + i) * P, (r0 + i + 1) * P)
-                    nc.tensor.matmul_mx(
-                        out=score[:, i, :],
-                        lhsT=k_codes[:, slots].bitcast(FP8X4),
-                        lhsT_scale=k_sc[r0 + i],
-                        rhs=q_codes[:, cols].bitcast(FP8X4),
-                        rhs_scale=q_sc[:, cols],
-                        start=True,
-                        stop=True,
-                    )
-                x = placed([P, together, width], F32, "x%s%d" % (name, r0), at_x and at_x + 4 * r0 * width)
-                ls_here = ls_all[:, cols].unsqueeze(1).to_broadcast([P, together, width])
-                nc.vector.tensor_tensor(x[:], score[:], ls_here, ALU.subtract)
-                for i in range(together):
-                    r = r0 + i
-                    nc.scalar.activation(y[:, r, :], x[:, i, :], ACT.Exp, bias=kb_col[:, r : r + 1])
-                done = r0 + together
-                if done in store_at:
-                    rows = slice(store_at[store_at.index(done) - 1], done)
-                    nc.sync.dma_start(y_rows[:, rows, cols], y[:, rows, :])
-            return y
+        ys = [placed([P, PACK, CHUNK], F32, "y%d" % c) for c in range(CHUNKS)]
 
-        def quantise_weights(y_bf, cols):
-            nc.vector.quantize_mx(
-                out=y_codes[:, cols].bitcast(FP8X4), scales=y_sc[:, cols], in_=y_bf[:].rearrange("p q r -> p (q r)")
-            )
+        def quantise_queries(c):
+            quantise(q_codes, q_sc[c][:], q_bf[c], c)
 
-        y_first = weigh(first, "_first", (0, 2, 4), AT_THIRD_RAW)
-        y_middle = weigh(middle, "_middle", (0, 1, 2, 4))
-        y_last = weigh(last, "_last", (0, 4))
-        first_bf = placed([P, CHUNK, PACK], BF16, "first_bf")
-        middle_bf = placed([P, HALF, PACK], BF16, "middle_bf")
-        last_bf = placed([P, CHUNK, PACK], BF16, "last_bf")
-        nc.gpsimd.tensor_scalar(first_bf[:], y_first[:].rearrange("p r q -> p q r"), 1.0, 0.0, ALU.mult, ALU.add)
-        nc.vector.tensor_copy(woven(middle_bf[:]), by_rows(y_middle[:]))
-        nc.vector.tensor_copy(woven(last_bf[:, 0:LAST_ON_VECTOR, :]), by_rows(y_last[:, :, 0:LAST_ON_VECTOR]))
-        nc.scalar.activation(woven(last_bf[:, LAST_ON_VECTOR:, :]), by_rows(y_last[:, :, LAST_ON_VECTOR:]), ACT.Copy)
-        quantise_weights(first_bf, first)
-        quantise_weights(middle_bf, middle)
-        nc.sync.dma_start(y_words[:, 0 : last.start], y_codes[:, 0 : last.start].bitcast(I32))
-        quantise_weights(last_bf, last)
-        nc.sync.dma_start(y_words[:, last], y_codes[:, last].bitcast(I32))
+        def weigh(bank):
+            c, r0 = bank // 2, 2 * (bank % 2)
+            cols = columns(c)
+            score = ps.tile([P, 2, CHUNK], F32, name="score", bufs=6)
+            for i in range(2):
+                slots = slice((r0 + i) * P, (r0 + i + 1) * P)
+                nc.tensor.matmul_mx(
+                    out=score[:, i, :],
+                    lhsT=k_codes[:, slots].bitcast(FP8X4),
+                    lhsT_scale=k_sc[:, r0 + i, :],
+                    rhs=q_codes[:, cols].bitcast(FP8X4),
+                    rhs_scale=q_sc[c][:],
+                    start=True,
+                    stop=True,
+                )
+            x = placed([P, 2, CHUNK], F32, "x%d" % bank, None if bank else AT_RAW[1])
+            ls_here = ls_all[:, cols].unsqueeze(1).to_broadcast([P, 2, CHUNK])
+            nc.vector.tensor_tensor(x[:], score[:], ls_here, ALU.subtract)
+            for i in range(2):
+                r = r0 + i
+                nc.scalar.activation(ys[c][:, r, :], x[:, i, :], ACT.Exp, bias=kb_col[:, r : r + 1])
+            if c == 0:
+                nc.sync.dma_start(y_rows[:, r0 : r0 + 2, cols], ys[c][:, r0 : r0 + 2, :])
+            elif r0:
+                nc.sync.dma_start(y_rows[:, :, cols], ys[c][:])
+
+        weave_on_scalar(q_bf[0], q_raw[0][:])
+        quantise_queries(0)
+        weave_on_vector(q_bf[1], q_raw[1][:])
+        weave_on_scalar(q_bf[2], q_raw[2][:])
+        weave_on_scalar(q_bf[3], q_raw[3][:])
+        quantise_queries(1)
+        for c in range(CHUNKS):
+            weigh(2 * c)
+            weigh(2 * c + 1)
+            if c + 2 < CHUNKS:
+                quantise_queries(c + 2)
+        last = CHUNKS - 1
+        y_bf = [placed([P, CHUNK, PACK], BF16, "y_bf%d" % c) for c in range(CHUNKS)]
+        weave_on_gpsimd(y_bf[0][:], ys[0][:])
+        weave_on_vector(y_bf[1][:], ys[1][:])
+        weave_on_vector(y_bf[2][:], ys[2][:])
+        weave_on_vector(y_bf[last][:, 0:LAST_ON_VECTOR, :], ys[last][:, :, 0:LAST_ON_VECTOR])
+        weave_on_scalar(y_bf[last][:, LAST_ON_VECTOR:, :], ys[last][:, :, LAST_ON_VECTOR:])
+        for c in range(last):
+            quantise(y_codes, y_sc[:, columns(c)], y_bf[c][:], c)
+        early = slice(0, last * CHUNK)
+        nc.sync.dma_start(y_words[:, early], y_codes[:, early].bitcast(I32))
+        quantise(y_codes, y_sc[:, columns(last)], y_bf[last][:], last)
         for r in range(4):
             queue = nc.sync if r % 2 else nc.scalar
             queue.dma_start(out_2[0, r:16:4, :].bitcast(I32), y_sc[r:P:32, :].bitcast(I32))
+            if r == 1:
+                nc.sync.dma_start(y_words[:, columns(last)], y_codes[:, columns(last)].bitcast(I32))

@@ -22,8 +22,8 @@ CHUNK = 128
 CHUNKS = NQ // CHUNK
 LAST_ON_VECTOR = 80
 KB_ROW = P - 1
-KEYS_AHEAD = 768
-AT_LS_ROWS = 960
+KEYS_AHEAD = 832
+AT_LS_ROWS, AT_ZEROS = 960, 10240
 AT_RAW = (2048, 8192, 4096, None)
 AT_Q_BF = (0, AT_RAW[0], 1024, AT_RAW[2])
 AT_Q_SC = (6144, 6272, 6144, 6272)
@@ -52,7 +52,7 @@ def tile_attend_plw_kb_topk_kernel(tc, qT, k_words, k_scales, kb, ls, offs, out_
 
         scale_pool = placed([P, T], U8, "scale_pool")
         nc.vector.memset(scale_pool[:].bitcast(I32), 0)
-        zeros = placed([P, P], F32, "zeros")
+        zeros = placed([P, P], F32, "zeros", AT_ZEROS)
         nc.vector.memset(zeros[:], 0.0)
         ident = placed([P, P], F32, "ident")
         nc.gpsimd.affine_select(
@@ -85,9 +85,20 @@ def tile_attend_plw_kb_topk_kernel(tc, qT, k_words, k_scales, kb, ls, offs, out_
             nc.sync.dma_start(q_raw[c][:], q_rows[:, :, columns(c)])
 
         kb_got = placed([P, N], F32, "kb_got")
-        nc.vector.tensor_copy(kb_got[:], kb_pool[:].indirect(offsets[:]))
+        nc.vector.tensor_copy(
+            kb_got[:].bitcast(U32).rearrange("p (r s) -> p s r", r=PACK), kb_pool[:].bitcast(U32).indirect(offsets[:])
+        )
         scale_got = placed([P, N], U8, "scale_got")
-        nc.vector.tensor_copy(scale_got[:], scale_pool[:].indirect(offsets[:]))
+        early_sc = placed([P, 2, P], U8, "early_sc")
+        late_sc = placed([P, 2, P], U8, "late_sc", AT_ZEROS)
+        k_sc = [early_sc[:, 0, :], early_sc[:, 1, :], late_sc[:, 0, :], late_sc[:, 1, :]]
+        by_place = scale_got[:].rearrange("p (s r) -> p r s", r=PACK)
+        for half in range(2):
+            listed = offsets[:, half * N // 32 : (half + 1) * N // 32]
+            nc.vector.tensor_copy(scale_got[:, half * N // 2 : (half + 1) * N // 2], scale_pool[:].indirect(listed))
+        for half in range(2):
+            places = slice(half * P // 2, (half + 1) * P // 2)
+            nc.vector.tensor_copy(early_sc[:, :, places], by_place[:, 0:2, places])
 
         q_codes = placed([P, NQ], U32, "q_codes")
         q_sc = [placed([P, CHUNK], U8, "q_sc%d" % c, AT_Q_SC[c]) for c in range(CHUNKS)]
@@ -118,16 +129,16 @@ def tile_attend_plw_kb_topk_kernel(tc, qT, k_words, k_scales, kb, ls, offs, out_
         )
         kb_ps = ps.tile([P, PACK, P], F32, name="kb_ps")
         for r in range(PACK):
-            nc.tensor.transpose(kb_ps[:, r, :], kb_got[:, r::PACK], ident[:])
+            nc.tensor.transpose(kb_ps[:, r, :], kb_got[:, r * P : (r + 1) * P], ident[:])
         kb_col = placed([P, PACK], F32, "kb_col")
         nc.scalar.copy(kb_col[:], kb_ps[:, :, KB_ROW])
 
-        k_sc = placed([P, PACK, P], U8, "k_sc")
-        nc.vector.tensor_copy(k_sc[:], scale_got[:].rearrange("p (s r) -> p r s", r=PACK))
         k_codes = placed([P, N], U32, "k_codes")
         nc.vector.tensor_copy(
             k_codes[:].rearrange("p (r s) -> p s r", r=PACK), word_pool[:].bitcast(U32).indirect(offsets[:])
         )
+
+        nc.vector.tensor_copy(late_sc[:], by_place[:, 2:4, :])
 
         y_rows = out_0.rearrange("(p r) q -> p r q", r=PACK)
         y_words = out_1[0].rearrange("p q u -> p (q u)").bitcast(I32)
@@ -148,7 +159,7 @@ def tile_attend_plw_kb_topk_kernel(tc, qT, k_words, k_scales, kb, ls, offs, out_
                 nc.tensor.matmul_mx(
                     out=score[:, i, :],
                     lhsT=k_codes[:, slots].bitcast(FP8X4),
-                    lhsT_scale=k_sc[:, r0 + i, :],
+                    lhsT_scale=k_sc[r0 + i],
                     rhs=q_codes[:, cols].bitcast(FP8X4),
                     rhs_scale=q_sc[c][:],
                     start=True,

@@ -22,7 +22,7 @@ CHUNK = 128
 CHUNKS = NQ // CHUNK
 LAST_ON_VECTOR = 80
 KB_ROW = P - 1
-KEYS_AHEAD = 832
+KEYS_AHEAD = 672
 AT_LS_ROWS, AT_ZEROS = 960, 10240
 AT_RAW = (2048, 8192, 4096, None)
 AT_Q_BF = (0, AT_RAW[0], 1024, AT_RAW[2])

@@ -22,11 +22,11 @@ CHUNK = 128
 CHUNKS = NQ // CHUNK
 LAST_ON_VECTOR = 80
 KB_ROW = P - 1
-KEYS_AHEAD = 672
-AT_LS_ROWS, AT_ZEROS = 960, 10240
-AT_RAW = (2048, 8192, 4096, None)
+AT_LS_ROWS = 960
+AT_RAW = (2048, 4096, 6144, 8192)
+AT_SCALE_POOL, AT_SCALE_GOT = AT_RAW[2] - 64, AT_RAW[3]
 AT_Q_BF = (0, AT_RAW[0], 1024, AT_RAW[2])
-AT_Q_SC = (6144, 6272, 6144, 6272)
+AT_Q_SC = (10240, 10368, 10240, 10368)
 
 
 def tile_attend_plw_kb_topk_kernel(tc, qT, k_words, k_scales, kb, ls, offs, out_0, out_1, out_2):
@@ -50,9 +50,9 @@ def tile_attend_plw_kb_topk_kernel(tc, qT, k_words, k_scales, kb, ls, offs, out_
         def columns(c):
             return slice(c * CHUNK, (c + 1) * CHUNK)
 
-        scale_pool = placed([P, T], U8, "scale_pool")
+        scale_pool = placed([P, T], U8, "scale_pool", AT_SCALE_POOL)
         nc.vector.memset(scale_pool[:].bitcast(I32), 0)
-        zeros = placed([P, P], F32, "zeros", AT_ZEROS)
+        zeros = placed([P, P], F32, "zeros")
         nc.vector.memset(zeros[:], 0.0)
         ident = placed([P, P], F32, "ident")
         nc.gpsimd.affine_select(
@@ -66,39 +66,33 @@ def tile_attend_plw_kb_topk_kernel(tc, qT, k_words, k_scales, kb, ls, offs, out_
         )
         kb_pool = placed([P, T], F32, "kb_pool")
         nc.vector.memset(kb_pool[0:KB_ROW, :], 0.0)
+        k_plane = placed([P, N], U8, "k_plane")
+        nc.vector.memset(k_plane[:].bitcast(I32), 0)
 
         q_rows = qT[0].rearrange("(p t) q -> p t q", t=PACK)
         q_raw = [placed([P, PACK, CHUNK], F32, "q_raw%d" % c, AT_RAW[c]) for c in range(CHUNKS)]
         offsets = sb.tile([P, N // 16], U16, name="offsets")
         nc.sync.dma_start(offsets[:], offs)
         nc.scalar.dma_start(kb_pool[KB_ROW:P, :], kb[0:1, :])
-        word_pool = placed([P, T], I32, "word_pool")
-        words = k_words[0].rearrange("p t r -> p (t r)").bitcast(I32)
-        nc.sync.dma_start(word_pool[:, 0:KEYS_AHEAD], words[:, 0:KEYS_AHEAD])
         ls_rows = placed([P, 32], F32, "ls_rows", AT_LS_ROWS)
         nc.sync.dma_start(ls_rows[:, 0:PACK], ls[0, 0].rearrange("(p j) -> p j", j=PACK))
-        for r in range(4):
-            queue = nc.scalar if r % 2 else nc.sync
-            queue.dma_start(scale_pool[r:P:32, :].bitcast(I32), k_scales[0, r:16:4, :].bitcast(I32))
-        nc.sync.dma_start(word_pool[:, KEYS_AHEAD:], words[:, KEYS_AHEAD:])
-        for c in range(CHUNKS):
+        nc.sync.dma_start(scale_pool[0:P:8, :].bitcast(I32), k_scales[0].bitcast(I32))
+        word_pool = placed([P, T], I32, "word_pool")
+        nc.sync.dma_start(word_pool[:], k_words[0].rearrange("p t r -> p (t r)").bitcast(I32))
+        nc.sync.dma_start(q_raw[0][:], q_rows[:, :, columns(0)])
+
+        scale_got = placed([P, N], U8, "scale_got", AT_SCALE_GOT)
+        nc.vector.tensor_copy(scale_got[:].rearrange("p (r s) -> p s r", r=PACK), scale_pool[:].indirect(offsets[:]))
+        for quad in range(0, P, 32):
+            nc.sync.dma_start(
+                k_plane[quad : quad + 4, :].bitcast(I32), scale_got[quad : quad + 32 : 8, :].bitcast(I32)
+            )
+        k_sc = [k_plane[:, r * P : (r + 1) * P] for r in range(PACK)]
+        for c in range(1, CHUNKS):
             nc.sync.dma_start(q_raw[c][:], q_rows[:, :, columns(c)])
 
         kb_got = placed([P, N], F32, "kb_got")
-        nc.vector.tensor_copy(
-            kb_got[:].bitcast(U32).rearrange("p (r s) -> p s r", r=PACK), kb_pool[:].bitcast(U32).indirect(offsets[:])
-        )
-        scale_got = placed([P, N], U8, "scale_got")
-        early_sc = placed([P, 2, P], U8, "early_sc")
-        late_sc = placed([P, 2, P], U8, "late_sc", AT_ZEROS)
-        k_sc = [early_sc[:, 0, :], early_sc[:, 1, :], late_sc[:, 0, :], late_sc[:, 1, :]]
-        by_place = scale_got[:].rearrange("p (s r) -> p r s", r=PACK)
-        for half in range(2):
-            listed = offsets[:, half * N // 32 : (half + 1) * N // 32]
-            nc.vector.tensor_copy(scale_got[:, half * N // 2 : (half + 1) * N // 2], scale_pool[:].indirect(listed))
-        for half in range(2):
-            places = slice(half * P // 2, (half + 1) * P // 2)
-            nc.vector.tensor_copy(early_sc[:, :, places], by_place[:, 0:2, places])
+        nc.scalar.activation(kb_got[:], kb_pool[:].indirect(offsets[:]), ACT.Copy)
 
         q_codes = placed([P, NQ], U32, "q_codes")
         q_sc = [placed([P, CHUNK], U8, "q_sc%d" % c, AT_Q_SC[c]) for c in range(CHUNKS)]
@@ -129,7 +123,7 @@ def tile_attend_plw_kb_topk_kernel(tc, qT, k_words, k_scales, kb, ls, offs, out_
         )
         kb_ps = ps.tile([P, PACK, P], F32, name="kb_ps")
         for r in range(PACK):
-            nc.tensor.transpose(kb_ps[:, r, :], kb_got[:, r * P : (r + 1) * P], ident[:])
+            nc.tensor.transpose(kb_ps[:, r, :], kb_got[:, r:N:PACK], ident[:])
         kb_col = placed([P, PACK], F32, "kb_col")
         nc.scalar.copy(kb_col[:], kb_ps[:, :, KB_ROW])
 
@@ -137,8 +131,6 @@ def tile_attend_plw_kb_topk_kernel(tc, qT, k_words, k_scales, kb, ls, offs, out_
         nc.vector.tensor_copy(
             k_codes[:].rearrange("p (r s) -> p s r", r=PACK), word_pool[:].bitcast(U32).indirect(offsets[:])
         )
-
-        nc.vector.tensor_copy(late_sc[:], by_place[:, 2:4, :])
 
         y_rows = out_0.rearrange("(p r) q -> p r q", r=PACK)
         y_words = out_1[0].rearrange("p q u -> p (q u)").bitcast(I32)

@@ -24,7 +24,7 @@ LAST_ON_VECTOR = 80
 KB_ROW = P - 1
 AT_LS_ROWS = 960
 AT_RAW = (2048, 4096, 6144, 8192)
-AT_SCALE_POOL, AT_SCALE_GOT = AT_RAW[2] - 64, AT_RAW[3]
+AT_SCALE_POOL = AT_RAW[3] - 64
 AT_Q_BF = (0, AT_RAW[0], 1024, AT_RAW[2])
 AT_Q_SC = (10240, 10368, 10240, 10368)
 
@@ -66,8 +66,6 @@ def tile_attend_plw_kb_topk_kernel(tc, qT, k_words, k_scales, kb, ls, offs, out_
         )
         kb_pool = placed([P, T], F32, "kb_pool")
         nc.vector.memset(kb_pool[0:KB_ROW, :], 0.0)
-        k_plane = placed([P, N], U8, "k_plane")
-        nc.vector.memset(k_plane[:].bitcast(I32), 0)
 
         q_rows = qT[0].rearrange("(p t) q -> p t q", t=PACK)
         q_raw = [placed([P, PACK, CHUNK], F32, "q_raw%d" % c, AT_RAW[c]) for c in range(CHUNKS)]
@@ -76,23 +74,28 @@ def tile_attend_plw_kb_topk_kernel(tc, qT, k_words, k_scales, kb, ls, offs, out_
         nc.scalar.dma_start(kb_pool[KB_ROW:P, :], kb[0:1, :])
         ls_rows = placed([P, 32], F32, "ls_rows", AT_LS_ROWS)
         nc.sync.dma_start(ls_rows[:, 0:PACK], ls[0, 0].rearrange("(p j) -> p j", j=PACK))
-        nc.sync.dma_start(scale_pool[0:P:8, :].bitcast(I32), k_scales[0].bitcast(I32))
+        nc.sync.dma_start(scale_pool[0:32:2, :].bitcast(I32), k_scales[0].bitcast(I32))
         word_pool = placed([P, T], I32, "word_pool")
         nc.sync.dma_start(word_pool[:], k_words[0].rearrange("p t r -> p (t r)").bitcast(I32))
-        nc.sync.dma_start(q_raw[0][:], q_rows[:, :, columns(0)])
+        for c in range(2):
+            nc.sync.dma_start(q_raw[c][:], q_rows[:, :, columns(c)])
 
-        scale_got = placed([P, N], U8, "scale_got", AT_SCALE_GOT)
+        scale_got = placed([P, N], U8, "scale_got")
         nc.vector.tensor_copy(scale_got[:].rearrange("p (r s) -> p s r", r=PACK), scale_pool[:].indirect(offsets[:]))
-        for quad in range(0, P, 32):
+        k_plane = placed([P, N], U8, "k_plane")
+        for quad in range(4):
             nc.sync.dma_start(
-                k_plane[quad : quad + 4, :].bitcast(I32), scale_got[quad : quad + 32 : 8, :].bitcast(I32)
+                k_plane[32 * quad : 32 * quad + 32, :].bitcast(I32),
+                scale_got[8 * quad : 8 * quad + 64 : 2, :].bitcast(I32),
             )
         k_sc = [k_plane[:, r * P : (r + 1) * P] for r in range(PACK)]
-        for c in range(1, CHUNKS):
+        for c in range(2, CHUNKS):
             nc.sync.dma_start(q_raw[c][:], q_rows[:, :, columns(c)])
 
         kb_got = placed([P, N], F32, "kb_got")
-        nc.scalar.activation(kb_got[:], kb_pool[:].indirect(offsets[:]), ACT.Copy)
+        nc.vector.tensor_copy(
+            kb_got[:].bitcast(U32).rearrange("p (r s) -> p s r", r=PACK), kb_pool[:].bitcast(U32).indirect(offsets[:])
+        )
 
         q_codes = placed([P, NQ], U32, "q_codes")
         q_sc = [placed([P, CHUNK], U8, "q_sc%d" % c, AT_Q_SC[c]) for c in range(CHUNKS)]
@@ -123,7 +126,7 @@ def tile_attend_plw_kb_topk_kernel(tc, qT, k_words, k_scales, kb, ls, offs, out_
         )
         kb_ps = ps.tile([P, PACK, P], F32, name="kb_ps")
         for r in range(PACK):
-            nc.tensor.transpose(kb_ps[:, r, :], kb_got[:, r:N:PACK], ident[:])
+            nc.tensor.transpose(kb_ps[:, r, :], kb_got[:, r * P : (r + 1) * P], ident[:])
         kb_col = placed([P, PACK], F32, "kb_col")
         nc.scalar.copy(kb_col[:], kb_ps[:, :, KB_ROW])
 

@@ -72,8 +72,10 @@ def tile_attend_plw_kb_topk_kernel(tc, qT, k_words, k_scales, kb, ls, offs, out_
         offsets = sb.tile([P, N // 16], U16, name="offsets")
         nc.sync.dma_start(offsets[:], offs)
         nc.scalar.dma_start(kb_pool[KB_ROW:P, :], kb[0:1, :])
+        ls_raw = placed([P, PACK], F32, "ls_raw")
+        nc.sync.dma_start(ls_raw[:], ls[0, 0].rearrange("(p j) -> p j", j=PACK))
         ls_rows = placed([P, 32], F32, "ls_rows", AT_LS_ROWS)
-        nc.sync.dma_start(ls_rows[:, 0:PACK], ls[0, 0].rearrange("(p j) -> p j", j=PACK))
+        nc.scalar.activation(ls_rows[:, 0:PACK], ls_raw[:], ACT.Copy, scale=-1.0)
         nc.sync.dma_start(scale_pool[0:32:2, :].bitcast(I32), k_scales[0].bitcast(I32))
         word_pool = placed([P, T], I32, "word_pool")
         nc.sync.dma_start(word_pool[:], k_words[0].rearrange("p t r -> p (t r)").bitcast(I32))
@@ -84,7 +86,8 @@ def tile_attend_plw_kb_topk_kernel(tc, qT, k_words, k_scales, kb, ls, offs, out_
         nc.vector.tensor_copy(scale_got[:].rearrange("p (r s) -> p s r", r=PACK), scale_pool[:].indirect(offsets[:]))
         k_plane = placed([P, N], U8, "k_plane")
         for quad in range(4):
-            nc.sync.dma_start(
+            queue = nc.scalar if quad % 2 else nc.sync
+            queue.dma_start(
                 k_plane[32 * quad : 32 * quad + 32, :].bitcast(I32),
                 scale_got[8 * quad : 8 * quad + 64 : 2, :].bitcast(I32),
             )
@@ -162,7 +165,7 @@ def tile_attend_plw_kb_topk_kernel(tc, qT, k_words, k_scales, kb, ls, offs, out_
                 )
             x = placed([P, 2, CHUNK], F32, "x%d" % bank, None if bank else AT_RAW[1])
             ls_here = ls_all[:, cols].unsqueeze(1).to_broadcast([P, 2, CHUNK])
-            nc.vector.tensor_tensor(x[:], score[:], ls_here, ALU.subtract)
+            nc.vector.tensor_tensor(x[:], score[:], ls_here, ALU.add)
             for i in range(2):
                 r = r0 + i
                 nc.scalar.activation(ys[c][:, r, :], x[:, i, :], ACT.Exp, bias=kb_col[:, r : r + 1])

@@ -21,11 +21,12 @@ PACK = 4
 CHUNK = 128
 CHUNKS = NQ // CHUNK
 LAST_ON_VECTOR = 80
+QUERIES_ON_VECTOR = 32
 KB_ROW = P - 1
 AT_LS_ROWS = 960
 AT_RAW = (2048, 4096, 6144, 8192)
 AT_SCALE_POOL = AT_RAW[3] - 64
-AT_Q_BF = (0, AT_RAW[0], 1024, AT_RAW[2])
+AT_Q_BF = (0, AT_RAW[0], 1024, 12288)
 AT_Q_SC = (10240, 10368, 10240, 10368)
 
 
@@ -100,7 +101,7 @@ def tile_attend_plw_kb_topk_kernel(tc, qT, k_words, k_scales, kb, ls, offs, out_
             kb_got[:].bitcast(U32).rearrange("p (r s) -> p s r", r=PACK), kb_pool[:].bitcast(U32).indirect(offsets[:])
         )
 
-        q_codes = placed([P, NQ], U32, "q_codes")
+        q_codes = [placed([P, CHUNK], U32, "q_codes%d" % c, None if c else AT_Q_BF[3])[:] for c in range(CHUNKS)]
         q_sc = [placed([P, CHUNK], U8, "q_sc%d" % c, AT_Q_SC[c]) for c in range(CHUNKS)]
         q_bf = [placed([P, CHUNK, PACK], BF16, "q_bf%d" % c, AT_Q_BF[c])[:] for c in range(CHUNKS)]
 
@@ -113,9 +114,9 @@ def tile_attend_plw_kb_topk_kernel(tc, qT, k_words, k_scales, kb, ls, offs, out_
         def weave_on_gpsimd(words_bf, rows):
             nc.gpsimd.tensor_scalar(words_bf, rows.rearrange("p r q -> p q r"), 1.0, 0.0, ALU.mult, ALU.add)
 
-        def quantise(codes, scales, words_bf, c):
+        def quantise(codes, scales, words_bf):
             nc.vector.quantize_mx(
-                out=codes[:, columns(c)].bitcast(FP8X4),
+                out=codes.bitcast(FP8X4),
                 scales=scales,
                 in_=words_bf.rearrange("p q t -> p (q t)"),
             )
@@ -146,7 +147,7 @@ def tile_attend_plw_kb_topk_kernel(tc, qT, k_words, k_scales, kb, ls, offs, out_
         ys = [placed([P, PACK, CHUNK], F32, "y%d" % c) for c in range(CHUNKS)]
 
         def quantise_queries(c):
-            quantise(q_codes, q_sc[c][:], q_bf[c], c)
+            quantise(q_codes[c], q_sc[c][:], q_bf[c])
 
         def weigh(bank):
             c, r0 = bank // 2, 2 * (bank % 2)
@@ -158,7 +159,7 @@ def tile_attend_plw_kb_topk_kernel(tc, qT, k_words, k_scales, kb, ls, offs, out_
                     out=score[:, i, :],
                     lhsT=k_codes[:, slots].bitcast(FP8X4),
                     lhsT_scale=k_sc[r0 + i],
-                    rhs=q_codes[:, cols].bitcast(FP8X4),
+                    rhs=q_codes[c].bitcast(FP8X4),
                     rhs_scale=q_sc[c][:],
                     start=True,
                     stop=True,
@@ -178,13 +179,15 @@ def tile_attend_plw_kb_topk_kernel(tc, qT, k_words, k_scales, kb, ls, offs, out_
         quantise_queries(0)
         weave_on_vector(q_bf[1], q_raw[1][:])
         weave_on_scalar(q_bf[2], q_raw[2][:])
-        weave_on_scalar(q_bf[3], q_raw[3][:])
+        weave_on_scalar(q_bf[3][:, QUERIES_ON_VECTOR:, :], q_raw[3][:, :, QUERIES_ON_VECTOR:])
         quantise_queries(1)
         for c in range(CHUNKS):
             weigh(2 * c)
             weigh(2 * c + 1)
             if c + 2 < CHUNKS:
                 quantise_queries(c + 2)
+            if c == 0:
+                weave_on_vector(q_bf[3][:, 0:QUERIES_ON_VECTOR, :], q_raw[3][:, :, 0:QUERIES_ON_VECTOR])
         last = CHUNKS - 1
         y_bf = [placed([P, CHUNK, PACK], BF16, "y_bf%d" % c) for c in range(CHUNKS)]
         weave_on_gpsimd(y_bf[0][:], ys[0][:])
@@ -193,10 +196,10 @@ def tile_attend_plw_kb_topk_kernel(tc, qT, k_words, k_scales, kb, ls, offs, out_
         weave_on_vector(y_bf[last][:, 0:LAST_ON_VECTOR, :], ys[last][:, :, 0:LAST_ON_VECTOR])
         weave_on_scalar(y_bf[last][:, LAST_ON_VECTOR:, :], ys[last][:, :, LAST_ON_VECTOR:])
         for c in range(last):
-            quantise(y_codes, y_sc[:, columns(c)], y_bf[c][:], c)
+            quantise(y_codes[:, columns(c)], y_sc[:, columns(c)], y_bf[c][:])
         early = slice(0, last * CHUNK)
         nc.sync.dma_start(y_words[:, early], y_codes[:, early].bitcast(I32))
-        quantise(y_codes, y_sc[:, columns(last)], y_bf[last][:], last)
+        quantise(y_codes[:, columns(last)], y_sc[:, columns(last)], y_bf[last][:])
         for r in range(4):
             queue = nc.sync if r % 2 else nc.scalar
             queue.dma_start(out_2[0, r:16:4, :].bitcast(I32), y_sc[r:P:32, :].bitcast(I32))

@@ -183,13 +183,13 @@ def tile_attend_plw_kb_topk_kernel(tc, qT, k_words, k_scales, kb, ls, offs, out_
         quantise_queries(1)
         for c in range(CHUNKS):
             weigh(2 * c)
+            if c == 1:
+                weave_on_vector(q_bf[3][:, 0:QUERIES_ON_VECTOR, :], q_raw[3][:, :, 0:QUERIES_ON_VECTOR])
             weigh(2 * c + 1)
             if c + 2 < CHUNKS:
                 quantise_queries(c + 2)
-            if c == 0:
-                weave_on_vector(q_bf[3][:, 0:QUERIES_ON_VECTOR, :], q_raw[3][:, :, 0:QUERIES_ON_VECTOR])
         last = CHUNKS - 1
-        y_bf = [placed([P, CHUNK, PACK], BF16, "y_bf%d" % c) for c in range(CHUNKS)]
+        y_bf = [placed([P, CHUNK, PACK], BF16, "y_bf%d" % c, None if c else AT_Q_BF[3]) for c in range(CHUNKS)]
         weave_on_gpsimd(y_bf[0][:], ys[0][:])
         weave_on_vector(y_bf[1][:], ys[1][:])
         weave_on_vector(y_bf[2][:], ys[2][:])

from contextlib import ExitStack

import concourse.mybir as mybir

N, T, D, NQ = 512, 2048, 512, 512
FLOPS = 2 * N * D * NQ
BYTES = 4 * D * NQ + D * T + 16 * T + 4 * T + 4 * NQ + 2 * 128 * (N // 16) + 4 * N * NQ + N * NQ + 16 * NQ

F32 = mybir.dt.float32
BF16 = mybir.dt.bfloat16
I32 = mybir.dt.int32
U32 = mybir.dt.uint32
U16 = mybir.dt.uint16
U8 = mybir.dt.uint8
FP8X4 = mybir.dt.float8_e4m3fn_x4
ACT = mybir.ActivationFunctionType
ALU = mybir.AluOpType

P = 128
PACK = 4
CHUNK = 128
CHUNKS = NQ // CHUNK
LAST_ON_VECTOR = 80
QUERIES_ON_VECTOR = 32
KB_ROW = P - 1
AT_LS_ROWS = 960
AT_RAW = (2048, 4096, 6144, 8192)
AT_SCALE_POOL = AT_RAW[3] - 64
AT_Q_BF = (0, AT_RAW[0], 1024, 12288)
AT_Q_SC = (10240, 10368, 10240, 10368)


def tile_attend_plw_kb_topk_kernel(tc, qT, k_words, k_scales, kb, ls, offs, out_0, out_1, out_2):
    nc = tc.nc
    with ExitStack() as ctx:
        sb = ctx.enter_context(tc.tile_pool(name="sb", bufs=1))
        shared = ctx.enter_context(tc.tile_pool(name="shared", bufs=1))
        ps = ctx.enter_context(tc.psum_pool(name="ps", bufs=1))

        def placed(shape, dtype, name, at=None):
            if at is None:
                return sb.tile(shape, dtype, name=name, align_bytes=64)
            return shared.tile(shape, dtype, name=name, align_bytes=64, offset=at)

        def woven(words):
            return words.rearrange("p (c i) t -> p c t i", i=4)

        def by_rows(rows):
            return rows.rearrange("p t (c i) -> p c t i", i=4)

        def columns(c):
            return slice(c * CHUNK, (c + 1) * CHUNK)

        scale_pool = placed([P, T], U8, "scale_pool", AT_SCALE_POOL)
        nc.vector.memset(scale_pool[:].bitcast(I32), 0)
        zeros = placed([P, P], F32, "zeros")
        nc.vector.memset(zeros[:], 0.0)
        ident = placed([P, P], F32, "ident")
        nc.gpsimd.affine_select(
            out=ident[:],
            in_=zeros[:],
            compare_op=ALU.not_equal,
            fill=1.0,
            base=0,
            pattern=[[-1, P]],
            channel_multiplier=1,
        )
        kb_pool = placed([P, T], F32, "kb_pool")
        nc.vector.memset(kb_pool[0:KB_ROW, :], 0.0)

        q_rows = qT[0].rearrange("(p t) q -> p t q", t=PACK)
        q_raw = [placed([P, PACK, CHUNK], F32, "q_raw%d" % c, AT_RAW[c]) for c in range(CHUNKS)]
        offsets = sb.tile([P, N // 16], U16, name="offsets")
        nc.sync.dma_start(offsets[:], offs)
        nc.scalar.dma_start(kb_pool[KB_ROW:P, :], kb[0:1, :])
        ls_raw = placed([P, PACK], F32, "ls_raw")
        nc.sync.dma_start(ls_raw[:], ls[0, 0].rearrange("(p j) -> p j", j=PACK))
        ls_rows = placed([P, 32], F32, "ls_rows", AT_LS_ROWS)
        nc.scalar.activation(ls_rows[:, 0:PACK], ls_raw[:], ACT.Copy, scale=-1.0)
        nc.sync.dma_start(scale_pool[0:32:2, :].bitcast(I32), k_scales[0].bitcast(I32))
        word_pool = placed([P, T], I32, "word_pool")
        nc.sync.dma_start(word_pool[:], k_words[0].rearrange("p t r -> p (t r)").bitcast(I32))
        for c in range(2):
            nc.sync.dma_start(q_raw[c][:], q_rows[:, :, columns(c)])

        scale_got = placed([P, N], U8, "scale_got")
        nc.vector.tensor_copy(scale_got[:].rearrange("p (r s) -> p s r", r=PACK), scale_pool[:].indirect(offsets[:]))
        k_plane = placed([P, N], U8, "k_plane")
        for quad in range(4):
            queue = nc.scalar if quad % 2 else nc.sync
            queue.dma_start(
                k_plane[32 * quad : 32 * quad + 32, :].bitcast(I32),
                scale_got[8 * quad : 8 * quad + 64 : 2, :].bitcast(I32),
            )
        k_sc = [k_plane[:, r * P : (r + 1) * P] for r in range(PACK)]
        for c in range(2, CHUNKS):
            nc.sync.dma_start(q_raw[c][:], q_rows[:, :, columns(c)])

        kb_got = placed([P, N], F32, "kb_got")
        nc.vector.tensor_copy(
            kb_got[:].bitcast(U32).rearrange("p (r s) -> p s r", r=PACK), kb_pool[:].bitcast(U32).indirect(offsets[:])
        )

        q_codes = [placed([P, CHUNK], U32, "q_codes%d" % c, None if c else AT_Q_BF[3])[:] for c in range(CHUNKS)]
        q_sc = [placed([P, CHUNK], U8, "q_sc%d" % c, AT_Q_SC[c]) for c in range(CHUNKS)]
        q_bf = [placed([P, CHUNK, PACK], BF16, "q_bf%d" % c, AT_Q_BF[c])[:] for c in range(CHUNKS)]

        def weave_on_scalar(words_bf, rows):
            nc.scalar.activation(woven(words_bf), by_rows(rows), ACT.Copy)

        def weave_on_vector(words_bf, rows):
            nc.vector.tensor_copy(woven(words_bf), by_rows(rows))

        def weave_on_gpsimd(words_bf, rows):
            nc.gpsimd.tensor_scalar(words_bf, rows.rearrange("p r q -> p q r"), 1.0, 0.0, ALU.mult, ALU.add)

        def quantise(codes, scales, words_bf):
            nc.vector.quantize_mx(
                out=codes.bitcast(FP8X4),
                scales=scales,
                in_=words_bf.rearrange("p q t -> p (q t)"),
            )

        ls_ps = ps.tile([P, PACK, P], F32, name="ls_ps")
        for j in range(PACK):
            nc.tensor.transpose(ls_ps[:, j, :], ls_rows[:, j : j + 1].to_broadcast([P, P]), ident[:])
        ls_all = placed([P, NQ], F32, "ls_all")
        nc.scalar.activation(
            ls_all[:].rearrange("p (c j) -> p c j", j=PACK), ls_ps[:].rearrange("p j c -> p c j"), ACT.Copy
        )
        kb_ps = ps.tile([P, PACK, P], F32, name="kb_ps")
        for r in range(PACK):
            nc.tensor.transpose(kb_ps[:, r, :], kb_got[:, r * P : (r + 1) * P], ident[:])
        kb_col = placed([P, PACK], F32, "kb_col")
        nc.scalar.copy(kb_col[:], kb_ps[:, :, KB_ROW])

        k_codes = placed([P, N], U32, "k_codes")
        nc.vector.tensor_copy(
            k_codes[:].rearrange("p (r s) -> p s r", r=PACK), word_pool[:].bitcast(U32).indirect(offsets[:])
        )

        y_rows = out_0.rearrange("(p r) q -> p r q", r=PACK)
        y_words = out_1[0].rearrange("p q u -> p (q u)").bitcast(I32)
        y_codes = placed([P, NQ], U32, "y_codes")
        y_sc = placed([P, NQ], U8, "y_sc")

        ys = [placed([P, PACK, CHUNK], F32, "y%d" % c) for c in range(CHUNKS)]

        def quantise_queries(c):
            quantise(q_codes[c], q_sc[c][:], q_bf[c])

        def weigh(bank):
            c, r0 = bank // 2, 2 * (bank % 2)
            cols = columns(c)
            score = ps.tile([P, 2, CHUNK], F32, name="score", bufs=6)
            for i in range(2):
                slots = slice((r0 + i) * P, (r0 + i + 1) * P)
                nc.tensor.matmul_mx(
                    out=score[:, i, :],
                    lhsT=k_codes[:, slots].bitcast(FP8X4),
                    lhsT_scale=k_sc[r0 + i],
                    rhs=q_codes[c].bitcast(FP8X4),
                    rhs_scale=q_sc[c][:],
                    start=True,
                    stop=True,
                )
            x = placed([P, 2, CHUNK], F32, "x%d" % bank, None if bank else AT_RAW[1])
            ls_here = ls_all[:, cols].unsqueeze(1).to_broadcast([P, 2, CHUNK])
            nc.vector.tensor_tensor(x[:], score[:], ls_here, ALU.add)
            for i in range(2):
                r = r0 + i
                nc.scalar.activation(ys[c][:, r, :], x[:, i, :], ACT.Exp, bias=kb_col[:, r : r + 1])
            if c == 0:
                nc.sync.dma_start(y_rows[:, r0 : r0 + 2, cols], ys[c][:, r0 : r0 + 2, :])
            elif r0:
                nc.sync.dma_start(y_rows[:, :, cols], ys[c][:])

        weave_on_scalar(q_bf[0], q_raw[0][:])
        quantise_queries(0)
        weave_on_vector(q_bf[1], q_raw[1][:])
        weave_on_scalar(q_bf[2], q_raw[2][:])
        weave_on_scalar(q_bf[3][:, QUERIES_ON_VECTOR:, :], q_raw[3][:, :, QUERIES_ON_VECTOR:])
        quantise_queries(1)
        for c in range(CHUNKS):
            weigh(2 * c)
            if c == 1:
                weave_on_vector(q_bf[3][:, 0:QUERIES_ON_VECTOR, :], q_raw[3][:, :, 0:QUERIES_ON_VECTOR])
            weigh(2 * c + 1)
            if c + 2 < CHUNKS:
                quantise_queries(c + 2)
        last = CHUNKS - 1
        y_bf = [placed([P, CHUNK, PACK], BF16, "y_bf%d" % c, None if c else AT_Q_BF[3]) for c in range(CHUNKS)]
        weave_on_gpsimd(y_bf[0][:], ys[0][:])
        weave_on_vector(y_bf[1][:], ys[1][:])
        weave_on_vector(y_bf[2][:], ys[2][:])
        weave_on_vector(y_bf[last][:, 0:LAST_ON_VECTOR, :], ys[last][:, :, 0:LAST_ON_VECTOR])
        weave_on_scalar(y_bf[last][:, LAST_ON_VECTOR:, :], ys[last][:, :, LAST_ON_VECTOR:])
        for c in range(last):
            quantise(y_codes[:, columns(c)], y_sc[:, columns(c)], y_bf[c][:])
        early = slice(0, last * CHUNK)
        nc.sync.dma_start(y_words[:, early], y_codes[:, early].bitcast(I32))
        quantise(y_codes[:, columns(last)], y_sc[:, columns(last)], y_bf[last][:])
        for r in range(4):
            queue = nc.sync if r % 2 else nc.scalar
            queue.dma_start(out_2[0, r:16:4, :].bitcast(I32), y_sc[r:P:32, :].bitcast(I32))
            if r == 1:
                nc.sync.dma_start(y_words[:, columns(last)], y_codes[:, columns(last)].bitcast(I32))
